import numpy as np
import ml_dtypes


def mxq(x, axis, fmt="e4m3"):
    dtype, down = {"e4m3": (ml_dtypes.float8_e4m3fn, 7), "e5m2": (ml_dtypes.float8_e5m2, 14)}[fmt]
    v = np.moveaxis(np.asarray(x, np.float32).astype(ml_dtypes.bfloat16).astype(np.float64), axis, -1)
    blocks = v.reshape(v.shape[:-1] + (-1, 32))
    amax = np.abs(blocks).max(-1, keepdims=True)
    byte = np.maximum(np.where(amax > 0, np.frexp(amax)[1] - 1 + 127, 0) - down, 1)
    scale = np.exp2(byte - 127.0)
    codes = (blocks / scale).astype(np.float32).astype(dtype).astype(np.float64)
    return np.moveaxis((codes * scale).reshape(v.shape), -1, axis)


WIDE = False


def mx_kscale(k):
    if not WIDE:
        return np.ones(k)
    levels = np.array([10, -10, 5, -5, 0])
    if k % 512:
        return np.exp2(np.random.permutation(np.resize(levels, k // 32))).repeat(32)
    a = np.empty((k // 512, 16))
    for p in range(k // 512):
        a[p, :8] = np.random.permutation(np.resize(levels, 8))
        for g in range(8):
            far = levels[np.abs(levels - a[p, g]) >= 10]
            a[p, g + 8] = far[np.random.randint(len(far))]
    return np.exp2(a.ravel()).repeat(32)


def f64(x):
    return np.asarray(x).astype(np.float64)


def striped(idx):
    return np.tile(idx.reshape(-1, 16).T, (8, 1)).astype(np.uint16)


def unstriped(offs):
    return offs[:16].T.reshape(-1).astype(np.int64)


E2M1 = np.array([0.0, 0.5, 1.0, 1.5, 2.0, 3.0, 4.0, 6.0, -0.0, -0.5, -1.0, -1.5, -2.0, -3.0, -4.0, -6.0])


def pack_weight(w, fmt):
    k, n = w.shape
    w = f64(np.asarray(w, np.float32).astype(ml_dtypes.bfloat16)).reshape(k // 32, 32, n)
    amax = np.abs(w).max(1)
    if fmt == "e4m3":
        byte = np.frexp(amax)[1] - 1 + 127 - 7
    else:
        mant, ex = np.frexp(amax / 6.0)
        byte = np.where(mant > 0.5, ex, ex - 1) + 127
    byte = np.clip(np.where(amax > 0, byte, 1), 1, 254)
    scaled = (w * np.exp2(127.0 - byte)[:, None, :]).reshape(k, n).astype(np.float32)
    by_word = np.ascontiguousarray(scaled.reshape(k // 512, 128, 4, n).transpose(0, 1, 3, 2))
    if fmt == "e4m3":
        words = by_word.astype(ml_dtypes.float8_e4m3fn).view(np.uint8)
    else:
        c = by_word.astype(ml_dtypes.float4_e2m1fn).view(np.uint8) & 0xF
        words = (c[..., 0::2] | (c[..., 1::2] << 4)).reshape(k // 512, 128, 2 * n)
    return np.ascontiguousarray(words), np.ascontiguousarray(byte.astype(np.uint8).reshape(k // 512, 16, n))


def unpack_weight(words, scales, fmt):
    g, _, n = scales.shape
    words = np.ascontiguousarray(words).reshape(g, 128, n, -1)
    if fmt == "e4m3":
        vals = words.view(ml_dtypes.float8_e4m3fn).astype(np.float64)
    else:
        nib = np.empty((g, 128, n, 4), np.uint8)
        nib[..., 0::2] = words & 0xF
        nib[..., 1::2] = words >> 4
        vals = E2M1[nib]
    vals = vals * np.repeat(np.exp2(scales.astype(np.float64) - 127.0), 8, axis=1)[..., None]
    return vals.transpose(0, 1, 3, 2).reshape(g * 512, n)


K, M, T, S = 1024, 512, 2048, 1024


def setup_inputs():
    n = np.random.standard_normal
    s = mx_kscale(K)[:, None]
    v = pack_weight(n((K, T)) * s, "e4m3")
    p_w4 = pack_weight(n((K, M)) / np.sqrt(K) / s, "e2m1")
    return {
        "tab_words": v[0],
        "tab_scales": v[1],
        "w4_words": p_w4[0],
        "w4_scales": p_w4[1],
        "dw": (n((K, M)) / np.sqrt(K) / s).astype(np.float32),
        "gT": n((M, T)).astype(np.float32),
        "offs": striped(np.random.permutation(T)[:S]),
    }


def reference(tab_words, tab_scales, w4_words, w4_scales, dw, gT, offs):
    tab_ = unpack_weight(tab_words, tab_scales, "e4m3")[:, unstriped(offs)]
    w4_ = unpack_weight(w4_words, w4_scales, "e2m1")
    dw_ = mxq(f64(dw), 0, "e4m3")
    y = w4_.T @ tab_ + dw_.T @ tab_
    return (y) * f64(gT)[:, unstriped(offs)]

@@ -1,0 +1,174 @@
+from contextlib import ExitStack
+
+import concourse.mybir as mybir
+
+K, M, T, S = 1024, 512, 2048, 1024
+FLOPS = 2 * 2 * K * M * S
+
+F32 = mybir.dt.float32
+BF16 = mybir.dt.bfloat16
+I32 = mybir.dt.int32
+U32 = mybir.dt.uint32
+U16 = mybir.dt.uint16
+U8 = mybir.dt.uint8
+FP8X4 = mybir.dt.float8_e4m3fn_x4
+FP4X4 = mybir.dt.float4_e2m1fn_x4
+MULT = mybir.AluOpType.mult
+
+P = 128
+PACK = 4
+PASSES = K // (P * PACK)
+NT = M // P
+HALF = 512
+HALVES = S // HALF
+
+
+def tile_list_tabgate_none_kernel(tc, tab_words, tab_scales, w4_words, w4_scales, dw, gT, offs, out):
+    nc = tc.nc
+    with ExitStack() as ctx:
+        keep = ctx.enter_context(tc.tile_pool(name="keep", bufs=1))
+        psum = ctx.enter_context(tc.psum_pool(name="psum", bufs=1))
+
+        def tile(shape, dtype, name, tag=None):
+            return keep.tile(shape, dtype, name=name, tag=tag or name, align_bytes=64)
+
+        scale_window = tile([P, T], U8, "scale_window", "slot0")
+        nc.gpsimd.memset(scale_window[:].bitcast(I32), 0)
+        w4_planes = tile([P, PASSES, M], U8, "w4_planes")
+        nc.vector.memset(w4_planes[:].rearrange("p a n -> p (a n)").bitcast(I32), 0)
+        tab_plane1 = tile([P, S], U8, "tab_plane1")
+        nc.vector.memset(tab_plane1[:].bitcast(I32), 0)
+
+        offsets = keep.tile([P, S // 16], U16, name="offsets")
+        nc.sync.dma_start(offsets[:], offs)
+
+        def picks(lo, hi):
+            return offsets[:, lo // 16 : hi // 16]
+
+        for q in range(4):
+            nc.sync.dma_start(scale_window[32 * q : 32 * q + 8, :].bitcast(I32), tab_scales[:, 4 * q : 4 * q + 4, :].bitcast(I32))
+
+        word_window = [tile([P, T], U32, "word_window%d" % a, "slot%d" % (1 + 2 * a)) for a in range(PASSES)]
+        dw_raw = [tile([P, PACK, M], F32, "dw_raw0", "slot2"), tile([P, PACK, M], F32, "dw_raw1")]
+        w4_codes = tile([P, PASSES, 2 * M], U8, "w4_codes")
+
+        def load_words(a):
+            nc.sync.dma_start(word_window[a][:].bitcast(I32), tab_words[a].rearrange("p t i -> p (t i)").bitcast(I32))
+
+        def load_dw(a):
+            nc.sync.dma_start(dw_raw[a][:], dw[a * 512 : (a + 1) * 512, :].rearrange("(p i) n -> p i n", i=PACK))
+
+        load_words(0)
+        nc.sync.dma_start(w4_codes[:].bitcast(I32), w4_words.rearrange("a p w -> p a w").bitcast(I32))
+        load_dw(0)
+        for q in range(4):
+            nc.sync.dma_start(
+                w4_planes[32 * q : 32 * q + 4, :, :].bitcast(I32),
+                w4_scales[:, 4 * q : 4 * q + 4, :].rearrange("a r n -> r a n").bitcast(I32),
+            )
+        load_words(1)
+        load_dw(1)
+
+        gate_window = {}
+
+        def load_gates(n):
+            gate_window[n] = tile([P, T], F32, "gate_window%d" % n, "slot%d" % n)
+            nc.sync.dma_start(gate_window[n][:], gT[n * P : (n + 1) * P, :])
+
+        tab_planes = tile([P, S], U8, "tab_planes")
+        tab_codes = [[tile([P, HALF], U32, "tab_codes%d_%d" % (a, h)) for h in range(HALVES)] for a in range(PASSES)]
+
+        def gather_scales(h):
+            nc.vector.tensor_copy(tab_planes[:, h * HALF : (h + 1) * HALF], scale_window[:].indirect(picks(h * HALF, (h + 1) * HALF)))
+
+        def gather_words(a, h):
+            nc.vector.tensor_copy(tab_codes[a][h][:], word_window[a][:].indirect(picks(h * HALF, (h + 1) * HALF)))
+
+        dw_codes = {}
+        dw_planes = {}
+        dw_bf = {}
+
+        def round_dw(a, lo, hi, on_vector):
+            g = tile([P, hi - lo, PACK], BF16, "dw_bf%d_%d" % (a, lo))
+            dw_bf[a, lo] = g
+            dst = g[:].rearrange("p (c j) i -> p c i j", j=4)
+            src = dw_raw[a][:, :, lo:hi].rearrange("p i (c j) -> p c i j", j=4)
+            if on_vector:
+                nc.vector.tensor_copy(dst, src)
+            else:
+                nc.scalar.copy(dst, src)
+
+        def quantize_dw(a, lo, hi):
+            codes = tile([P, hi - lo], U32, "dw_codes%d_%d" % (a, lo))
+            plane = tile([P, hi - lo], U8, "dw_plane%d_%d" % (a, lo))
+            nc.vector.quantize_mx(out=codes[:].bitcast(FP8X4), scales=plane[:], in_=dw_bf[a, lo][:].rearrange("p c i -> p (c i)"))
+            for n in range(lo // P, hi // P):
+                dw_codes[a, n] = codes[:, n * P - lo : (n + 1) * P - lo]
+                dw_planes[a, n] = plane[:, n * P - lo : (n + 1) * P - lo]
+
+        acc = [[psum.tile([P, HALF], F32, name="acc%d_%d" % (n, h)) for h in range(HALVES)] for n in range(NT)]
+
+        def w4_pass(a, n, h, start, stop):
+            plane = tab_planes if a == 0 else tab_plane1
+            nc.tensor.matmul_mx(
+                out=acc[n][h][:],
+                lhsT=w4_codes[:, a, 2 * n * P : 2 * (n + 1) * P].bitcast(FP4X4),
+                lhsT_scale=w4_planes[:, a, n * P : (n + 1) * P],
+                rhs=tab_codes[a][h][:].bitcast(FP8X4),
+                rhs_scale=plane[:, h * HALF : (h + 1) * HALF],
+                start=start,
+                stop=stop,
+            )
+
+        def dw_pass(a, n, h, start, stop):
+            nc.tensor.matmul_mx(
+                out=acc[n][h][:],
+                lhsT=dw_codes[a, n].bitcast(FP8X4),
+                lhsT_scale=dw_planes[a, n],
+                rhs=tab_codes[a][h][:].bitcast(FP8X4),
+                rhs_scale=tab_planes[4 * a :, h * HALF : (h + 1) * HALF],
+                start=start,
+                stop=stop,
+            )
+
+        for h in range(HALVES):
+            gather_scales(h)
+            gather_words(0, h)
+        nc.sync.dma_start(tab_plane1[0:112, :].bitcast(I32), tab_planes[4:116, :].bitcast(I32))
+        load_gates(0)
+        load_gates(1)
+        for lo in (0, 256):
+            round_dw(0, lo, lo + 256, False)
+        load_gates(2)
+        for h in range(HALVES):
+            for n in range(NT):
+                w4_pass(0, n, h, True, False)
+        quantize_dw(0, 0, 256)
+        gather_words(1, 0)
+        quantize_dw(0, 256, 512)
+        gather_words(1, 1)
+        load_gates(3)
+        for n in range(NT):
+            for h in range(HALVES):
+                dw_pass(0, n, h, False, False)
+        for n in range(NT):
+            round_dw(1, n * P, (n + 1) * P, n < 2)
+        for n in range(NT):
+            quantize_dw(1, n * P, (n + 1) * P)
+
+        for n in range(NT):
+            result = tile([P, S], F32, "result%d" % n)
+            for h in range(HALVES):
+                dw_pass(1, n, h, False, False)
+                w4_pass(1, n, h, False, True)
+                y = tile([P, HALF], F32, "y%d_%d" % (n, h))
+                nc.scalar.copy(y[:], acc[n][h][:])
+                last = n == NT - 1 and h == HALVES - 1
+                piece = HALF // 2 if last else HALF
+                for c in range(0, HALF, piece):
+                    lo = h * HALF + c
+                    nc.vector.tensor_tensor(result[:, lo : lo + piece], gate_window[n][:].indirect(picks(lo, lo + piece)), y[:, c : c + piece], MULT)
+                    if n == NT - 1:
+                        nc.sync.dma_start(out[n * P : (n + 1) * P, lo : lo + piece], result[:, lo : lo + piece])
+            if n < NT - 1:
+                nc.sync.dma_start(out[n * P : (n + 1) * P, :], result[:])

@@ -21,6 +21,7 @@ PASSES = K // (P * PACK)
 NT = M // P
 HALF = 512
 HALVES = S // HALF
+EARLY = 3
 
 
 def tile_list_tabgate_none_kernel(tc, tab_words, tab_scales, w4_words, w4_scales, dw, gT, offs, out):
@@ -33,7 +34,7 @@ def tile_list_tabgate_none_kernel(tc, tab_words, tab_scales, w4_words, w4_scales
             return keep.tile(shape, dtype, name=name, tag=tag or name, align_bytes=64)
 
         scale_window = tile([P, T], U8, "scale_window", "slot0")
-        nc.gpsimd.memset(scale_window[:].bitcast(I32), 0)
+        nc.vector.memset(scale_window[:].bitcast(I32), 0)
         w4_planes = tile([P, PASSES, M], U8, "w4_planes")
         nc.vector.memset(w4_planes[:].rearrange("p a n -> p (a n)").bitcast(I32), 0)
         tab_plane1 = tile([P, S], U8, "tab_plane1")
@@ -41,6 +42,8 @@ def tile_list_tabgate_none_kernel(tc, tab_words, tab_scales, w4_words, w4_scales
 
         offsets = keep.tile([P, S // 16], U16, name="offsets")
         nc.sync.dma_start(offsets[:], offs)
+        w4_codes = tile([P, PASSES, 2 * M], U8, "w4_codes")
+        nc.sync.dma_start(w4_codes[:].bitcast(I32), w4_words.rearrange("a p w -> p a w").bitcast(I32))
 
         def picks(lo, hi):
             return offsets[:, lo // 16 : hi // 16]
@@ -50,7 +53,6 @@ def tile_list_tabgate_none_kernel(tc, tab_words, tab_scales, w4_words, w4_scales
 
         word_window = [tile([P, T], U32, "word_window%d" % a, "slot%d" % (1 + 2 * a)) for a in range(PASSES)]
         dw_raw = [tile([P, PACK, M], F32, "dw_raw0", "slot2"), tile([P, PACK, M], F32, "dw_raw1")]
-        w4_codes = tile([P, PASSES, 2 * M], U8, "w4_codes")
 
         def load_words(a):
             nc.sync.dma_start(word_window[a][:].bitcast(I32), tab_words[a].rearrange("p t i -> p (t i)").bitcast(I32))
@@ -59,7 +61,6 @@ def tile_list_tabgate_none_kernel(tc, tab_words, tab_scales, w4_words, w4_scales
             nc.sync.dma_start(dw_raw[a][:], dw[a * 512 : (a + 1) * 512, :].rearrange("(p i) n -> p i n", i=PACK))
 
         load_words(0)
-        nc.sync.dma_start(w4_codes[:].bitcast(I32), w4_words.rearrange("a p w -> p a w").bitcast(I32))
         load_dw(0)
         for q in range(4):
             nc.sync.dma_start(
@@ -77,9 +78,6 @@ def tile_list_tabgate_none_kernel(tc, tab_words, tab_scales, w4_words, w4_scales
 
         tab_planes = tile([P, S], U8, "tab_planes")
         tab_codes = [[tile([P, HALF], U32, "tab_codes%d_%d" % (a, h)) for h in range(HALVES)] for a in range(PASSES)]
-
-        def gather_scales(h):
-            nc.vector.tensor_copy(tab_planes[:, h * HALF : (h + 1) * HALF], scale_window[:].indirect(picks(h * HALF, (h + 1) * HALF)))
 
         def gather_words(a, h):
             nc.vector.tensor_copy(tab_codes[a][h][:], word_window[a][:].indirect(picks(h * HALF, (h + 1) * HALF)))
@@ -106,7 +104,10 @@ def tile_list_tabgate_none_kernel(tc, tab_words, tab_scales, w4_words, w4_scales
                 dw_codes[a, n] = codes[:, n * P - lo : (n + 1) * P - lo]
                 dw_planes[a, n] = plane[:, n * P - lo : (n + 1) * P - lo]
 
-        acc = [[psum.tile([P, HALF], F32, name="acc%d_%d" % (n, h)) for h in range(HALVES)] for n in range(NT)]
+        acc = {}
+
+        def open_banks(n):
+            acc[n] = [psum.tile([P, HALF], F32, name="acc%d_%d" % (n, h), tag="bank%d_%d" % (n % EARLY, h)) for h in range(HALVES)]
 
         def w4_pass(a, n, h, start, stop):
             plane = tab_planes if a == 0 else tab_plane1
@@ -131,8 +132,8 @@ def tile_list_tabgate_none_kernel(tc, tab_words, tab_scales, w4_words, w4_scales
                 stop=stop,
             )
 
+        nc.vector.tensor_copy(tab_planes[:], scale_window[:].indirect(offsets[:]))
         for h in range(HALVES):
-            gather_scales(h)
             gather_words(0, h)
         nc.sync.dma_start(tab_plane1[0:112, :].bitcast(I32), tab_planes[4:116, :].bitcast(I32))
         load_gates(0)
@@ -140,35 +141,41 @@ def tile_list_tabgate_none_kernel(tc, tab_words, tab_scales, w4_words, w4_scales
         for lo in (0, 256):
             round_dw(0, lo, lo + 256, False)
         load_gates(2)
+        for n in range(EARLY):
+            open_banks(n)
         for h in range(HALVES):
-            for n in range(NT):
+            for n in range(EARLY):
                 w4_pass(0, n, h, True, False)
         quantize_dw(0, 0, 256)
         gather_words(1, 0)
         quantize_dw(0, 256, 512)
         gather_words(1, 1)
         load_gates(3)
-        for n in range(NT):
+        for n in range(EARLY):
             for h in range(HALVES):
                 dw_pass(0, n, h, False, False)
         for n in range(NT):
-            round_dw(1, n * P, (n + 1) * P, n < 2)
+            round_dw(1, n * P, (n + 1) * P, n % 2 == 1)
         for n in range(NT):
             quantize_dw(1, n * P, (n + 1) * P)
 
         for n in range(NT):
+            if n >= EARLY:
+                open_banks(n)
             result = tile([P, S], F32, "result%d" % n)
+            y = tile([P, S], F32, "y%d" % n)
             for h in range(HALVES):
-                dw_pass(1, n, h, False, False)
-                w4_pass(1, n, h, False, True)
-                y = tile([P, HALF], F32, "y%d_%d" % (n, h))
-                nc.scalar.copy(y[:], acc[n][h][:])
-                last = n == NT - 1 and h == HALVES - 1
-                piece = HALF // 2 if last else HALF
-                for c in range(0, HALF, piece):
-                    lo = h * HALF + c
-                    nc.vector.tensor_tensor(result[:, lo : lo + piece], gate_window[n][:].indirect(picks(lo, lo + piece)), y[:, c : c + piece], MULT)
-                    if n == NT - 1:
-                        nc.sync.dma_start(out[n * P : (n + 1) * P, lo : lo + piece], result[:, lo : lo + piece])
+                if n >= EARLY:
+                    w4_pass(0, n, h, True, False)
+                    dw_pass(0, n, h, False, False)
+                w4_pass(1, n, h, False, False)
+                dw_pass(1, n, h, False, True)
+                nc.scalar.copy(y[:, h * HALF : (h + 1) * HALF], acc[n][h][:])
+            lo = 0
+            for piece in ([512, 512], [1024], [1024], [512, 256, 256])[n]:
+                nc.vector.tensor_tensor(result[:, lo : lo + piece], gate_window[n][:].indirect(picks(lo, lo + piece)), y[:, lo : lo + piece], MULT)
+                if n == NT - 1:
+                    nc.sync.dma_start(out[n * P : (n + 1) * P, lo : lo + piece], result[:, lo : lo + piece])
+                lo = lo + piece
             if n < NT - 1:
                 nc.sync.dma_start(out[n * P : (n + 1) * P, :], result[:])

@@ -48,8 +48,8 @@ def tile_list_tabgate_none_kernel(tc, tab_words, tab_scales, w4_words, w4_scales
         def picks(lo, hi):
             return offsets[:, lo // 16 : hi // 16]
 
-        for q in range(4):
-            nc.sync.dma_start(scale_window[32 * q : 32 * q + 8, :].bitcast(I32), tab_scales[:, 4 * q : 4 * q + 4, :].bitcast(I32))
+        for r in range(4):
+            nc.sync.dma_start(scale_window[r:P:16, :].bitcast(I32), tab_scales[:, r:16:4, :].rearrange("a q t -> q a t").bitcast(I32))
 
         word_window = [tile([P, T], U32, "word_window%d" % a, "slot%d" % (1 + 2 * a)) for a in range(PASSES)]
         dw_raw = [tile([P, PACK, M], F32, "dw_raw0", "slot2"), tile([P, PACK, M], F32, "dw_raw1")]
@@ -127,7 +127,7 @@ def tile_list_tabgate_none_kernel(tc, tab_words, tab_scales, w4_words, w4_scales
                 lhsT=dw_codes[a, n].bitcast(FP8X4),
                 lhsT_scale=dw_planes[a, n],
                 rhs=tab_codes[a][h][:].bitcast(FP8X4),
-                rhs_scale=tab_planes[4 * a :, h * HALF : (h + 1) * HALF],
+                rhs_scale=(tab_planes if a == 0 else tab_plane1)[:, h * HALF : (h + 1) * HALF],
                 start=start,
                 stop=stop,
             )
@@ -135,7 +135,7 @@ def tile_list_tabgate_none_kernel(tc, tab_words, tab_scales, w4_words, w4_scales
         nc.vector.tensor_copy(tab_planes[:], scale_window[:].indirect(offsets[:]))
         for h in range(HALVES):
             gather_words(0, h)
-        nc.sync.dma_start(tab_plane1[0:112, :].bitcast(I32), tab_planes[4:116, :].bitcast(I32))
+        nc.sync.dma_start(tab_plane1[0:112, :].bitcast(I32), tab_planes[16:128, :].bitcast(I32))
         load_gates(0)
         load_gates(1)
         for lo in (0, 256):
@@ -155,9 +155,10 @@ def tile_list_tabgate_none_kernel(tc, tab_words, tab_scales, w4_words, w4_scales
             for h in range(HALVES):
                 dw_pass(0, n, h, False, False)
         for n in range(NT):
-            round_dw(1, n * P, (n + 1) * P, n % 2 == 1)
-        for n in range(NT):
-            quantize_dw(1, n * P, (n + 1) * P)
+            round_dw(1, n * P, (n + 1) * P, n % 2 == 0)
+            if n > 0:
+                quantize_dw(1, (n - 1) * P, n * P)
+        quantize_dw(1, (NT - 1) * P, NT * P)
 
         for n in range(NT):
             if n >= EARLY:

@@ -21,7 +21,7 @@ PASSES = K // (P * PACK)
 NT = M // P
 HALF = 512
 HALVES = S // HALF
-EARLY = 3
+PAIR = 2 * P
 
 
 def tile_list_tabgate_none_kernel(tc, tab_words, tab_scales, w4_words, w4_scales, dw, gT, offs, out):
@@ -41,40 +41,39 @@ def tile_list_tabgate_none_kernel(tc, tab_words, tab_scales, w4_words, w4_scales
         nc.vector.memset(tab_plane1[:].bitcast(I32), 0)
 
         offsets = keep.tile([P, S // 16], U16, name="offsets")
-        nc.sync.dma_start(offsets[:], offs)
         w4_codes = tile([P, PASSES, 2 * M], U8, "w4_codes")
-        nc.sync.dma_start(w4_codes[:].bitcast(I32), w4_words.rearrange("a p w -> p a w").bitcast(I32))
+        word_window = [tile([P, T], U32, "word_window%d" % a, "slot%d" % (1 + a)) for a in range(PASSES)]
+        gate_window = {}
+        dw_raw = {}
 
         def picks(lo, hi):
             return offsets[:, lo // 16 : hi // 16]
 
-        for r in range(4):
-            nc.sync.dma_start(scale_window[r:P:16, :].bitcast(I32), tab_scales[:, r:16:4, :].rearrange("a q t -> q a t").bitcast(I32))
-
-        word_window = [tile([P, T], U32, "word_window%d" % a, "slot%d" % (1 + 2 * a)) for a in range(PASSES)]
-        dw_raw = [tile([P, PACK, M], F32, "dw_raw0", "slot2"), tile([P, PACK, M], F32, "dw_raw1")]
-
         def load_words(a):
             nc.sync.dma_start(word_window[a][:].bitcast(I32), tab_words[a].rearrange("p t i -> p (t i)").bitcast(I32))
 
-        def load_dw(a):
-            nc.sync.dma_start(dw_raw[a][:], dw[a * 512 : (a + 1) * 512, :].rearrange("(p i) n -> p i n", i=PACK))
+        def load_gates(n, slot):
+            gate_window[n] = tile([P, T], F32, "gate_window%d" % n, "slot%d" % slot)
+            nc.sync.dma_start(gate_window[n][:], gT[n * P : (n + 1) * P, :])
 
+        def load_dw(a, lo, hi, slot):
+            raw = tile([P, PACK, hi - lo], F32, "dw_raw%d_%d" % (a, lo), "slot%d" % slot)
+            nc.sync.dma_start(raw[:], dw[a * 512 : (a + 1) * 512, lo:hi].rearrange("(p i) n -> p i n", i=PACK))
+            for n in range(lo // P, hi // P):
+                dw_raw[a, n] = (raw, lo)
+
+        nc.sync.dma_start(offsets[:], offs)
+        nc.sync.dma_start(w4_codes[:].bitcast(I32), w4_words.rearrange("a p w -> p a w").bitcast(I32))
+        for r in range(4):
+            nc.sync.dma_start(scale_window[r:P:16, :].bitcast(I32), tab_scales[:, r:16:4, :].rearrange("a q t -> q a t").bitcast(I32))
         load_words(0)
-        load_dw(0)
         for q in range(4):
             nc.sync.dma_start(
                 w4_planes[32 * q : 32 * q + 4, :, :].bitcast(I32),
                 w4_scales[:, 4 * q : 4 * q + 4, :].rearrange("a r n -> r a n").bitcast(I32),
             )
         load_words(1)
-        load_dw(1)
-
-        gate_window = {}
-
-        def load_gates(n):
-            gate_window[n] = tile([P, T], F32, "gate_window%d" % n, "slot%d" % n)
-            nc.sync.dma_start(gate_window[n][:], gT[n * P : (n + 1) * P, :])
+        load_dw(1, 0, PAIR, 3)
 
         tab_planes = tile([P, S], U8, "tab_planes")
         tab_codes = [[tile([P, HALF], U32, "tab_codes%d_%d" % (a, h)) for h in range(HALVES)] for a in range(PASSES)]
@@ -86,18 +85,19 @@ def tile_list_tabgate_none_kernel(tc, tab_words, tab_scales, w4_words, w4_scales
         dw_planes = {}
         dw_bf = {}
 
-        def round_dw(a, lo, hi, on_vector):
-            g = tile([P, hi - lo, PACK], BF16, "dw_bf%d_%d" % (a, lo))
+        def round_dw(a, lo, hi, on_vector, tag=None):
+            g = tile([P, hi - lo, PACK], BF16, "dw_bf%d_%d" % (a, lo), tag)
             dw_bf[a, lo] = g
             dst = g[:].rearrange("p (c j) i -> p c i j", j=4)
-            src = dw_raw[a][:, :, lo:hi].rearrange("p i (c j) -> p c i j", j=4)
+            raw, base = dw_raw[a, lo // P]
+            src = raw[:, :, lo - base : hi - base].rearrange("p i (c j) -> p c i j", j=4)
             if on_vector:
                 nc.vector.tensor_copy(dst, src)
             else:
                 nc.scalar.copy(dst, src)
 
-        def quantize_dw(a, lo, hi):
-            codes = tile([P, hi - lo], U32, "dw_codes%d_%d" % (a, lo))
+        def quantize_dw(a, lo, hi, tag=None):
+            codes = tile([P, hi - lo], U32, "dw_codes%d_%d" % (a, lo), tag)
             plane = tile([P, hi - lo], U8, "dw_plane%d_%d" % (a, lo))
             nc.vector.quantize_mx(out=codes[:].bitcast(FP8X4), scales=plane[:], in_=dw_bf[a, lo][:].rearrange("p c i -> p (c i)"))
             for n in range(lo // P, hi // P):
@@ -106,8 +106,10 @@ def tile_list_tabgate_none_kernel(tc, tab_words, tab_scales, w4_words, w4_scales
 
         acc = {}
 
-        def open_banks(n):
-            acc[n] = [psum.tile([P, HALF], F32, name="acc%d_%d" % (n, h), tag="bank%d_%d" % (n % EARLY, h)) for h in range(HALVES)]
+        def open_tile(n):
+            acc[n] = [psum.tile([P, HALF], F32, name="acc%d_%d" % (n, h), tag="bank%d_%d" % (n % 2, h)) for h in range(HALVES)]
+            for h in range(HALVES):
+                w4_pass(0, n, h, True, False)
 
         def w4_pass(a, n, h, start, stop):
             plane = tab_planes if a == 0 else tab_plane1
@@ -132,51 +134,53 @@ def tile_list_tabgate_none_kernel(tc, tab_words, tab_scales, w4_words, w4_scales
                 stop=stop,
             )
 
-        nc.vector.tensor_copy(tab_planes[:], scale_window[:].indirect(offsets[:]))
-        for h in range(HALVES):
-            gather_words(0, h)
-        nc.sync.dma_start(tab_plane1[0:112, :].bitcast(I32), tab_planes[16:128, :].bitcast(I32))
-        load_gates(0)
-        load_gates(1)
-        for lo in (0, 256):
-            round_dw(0, lo, lo + 256, False)
-        load_gates(2)
-        for n in range(EARLY):
-            open_banks(n)
-        for h in range(HALVES):
-            for n in range(EARLY):
-                w4_pass(0, n, h, True, False)
-        quantize_dw(0, 0, 256)
-        gather_words(1, 0)
-        quantize_dw(0, 256, 512)
-        gather_words(1, 1)
-        load_gates(3)
-        for n in range(EARLY):
-            for h in range(HALVES):
-                dw_pass(0, n, h, False, False)
-        for n in range(NT):
-            round_dw(1, n * P, (n + 1) * P, n % 2 == 0)
-            if n > 0:
-                quantize_dw(1, (n - 1) * P, n * P)
-        quantize_dw(1, (NT - 1) * P, NT * P)
-
-        for n in range(NT):
-            if n >= EARLY:
-                open_banks(n)
+        def finish(n, pieces, then=None):
             result = tile([P, S], F32, "result%d" % n)
             y = tile([P, S], F32, "y%d" % n)
             for h in range(HALVES):
-                if n >= EARLY:
-                    w4_pass(0, n, h, True, False)
-                    dw_pass(0, n, h, False, False)
                 w4_pass(1, n, h, False, False)
-                dw_pass(1, n, h, False, True)
+                dw_pass(1 if n < 2 else 0, n, h, False, False)
+                dw_pass(0 if n < 2 else 1, n, h, False, True)
                 nc.scalar.copy(y[:, h * HALF : (h + 1) * HALF], acc[n][h][:])
             lo = 0
-            for piece in ([512, 512], [1024], [1024], [512, 256, 256])[n]:
+            for piece in pieces:
                 nc.vector.tensor_tensor(result[:, lo : lo + piece], gate_window[n][:].indirect(picks(lo, lo + piece)), y[:, lo : lo + piece], MULT)
                 if n == NT - 1:
                     nc.sync.dma_start(out[n * P : (n + 1) * P, lo : lo + piece], result[:, lo : lo + piece])
                 lo = lo + piece
+            if then is not None:
+                then()
             if n < NT - 1:
                 nc.sync.dma_start(out[n * P : (n + 1) * P, :], result[:])
+
+        def prepare_dw(a, n, on_vector):
+            round_dw(a, n * P, (n + 1) * P, on_vector)
+            quantize_dw(a, n * P, (n + 1) * P)
+
+        nc.vector.tensor_copy(tab_planes[:], scale_window[:].indirect(offsets[:]))
+        nc.sync.dma_start(tab_plane1[0:112, :].bitcast(I32), tab_planes[16:128, :].bitcast(I32))
+        load_dw(0, 0, M, 0)
+        for h in range(HALVES):
+            gather_words(0, h)
+        load_gates(0, 1)
+        for h in range(HALVES):
+            gather_words(1, h)
+        load_dw(1, PAIR, M, 2)
+        round_dw(1, 0, PAIR, False)
+        load_gates(1, 3)
+        quantize_dw(1, 0, PAIR)
+        for n in range(NT):
+            round_dw(0, n * P, (n + 1) * P, n % 3 == 0)
+        for n in range(NT):
+            quantize_dw(0, n * P, (n + 1) * P)
+        load_gates(2, 0)
+        open_tile(0)
+        open_tile(1)
+        finish(0, [512, 512], lambda: load_gates(3, 1))
+        finish(1, [1024])
+        for n in range(2, NT):
+            prepare_dw(1, n, False)
+        open_tile(2)
+        finish(2, [1024])
+        open_tile(3)
+        finish(3, [512, 256, 256])

@@ -67,12 +67,12 @@ def tile_list_tabgate_none_kernel(tc, tab_words, tab_scales, w4_words, w4_scales
         for r in range(4):
             nc.sync.dma_start(scale_window[r:P:16, :].bitcast(I32), tab_scales[:, r:16:4, :].rearrange("a q t -> q a t").bitcast(I32))
         load_words(0)
+        load_words(1)
         for q in range(4):
             nc.sync.dma_start(
                 w4_planes[32 * q : 32 * q + 4, :, :].bitcast(I32),
                 w4_scales[:, 4 * q : 4 * q + 4, :].rearrange("a r n -> r a n").bitcast(I32),
             )
-        load_words(1)
         load_dw(1, 0, PAIR, 3)
 
         tab_planes = tile([P, S], U8, "tab_planes")
@@ -134,7 +134,7 @@ def tile_list_tabgate_none_kernel(tc, tab_words, tab_scales, w4_words, w4_scales
                 stop=stop,
             )
 
-        def finish(n, pieces, then=None):
+        def finish(n, pieces):
             result = tile([P, S], F32, "result%d" % n)
             y = tile([P, S], F32, "y%d" % n)
             for h in range(HALVES):
@@ -148,8 +148,6 @@ def tile_list_tabgate_none_kernel(tc, tab_words, tab_scales, w4_words, w4_scales
                 if n == NT - 1:
                     nc.sync.dma_start(out[n * P : (n + 1) * P, lo : lo + piece], result[:, lo : lo + piece])
                 lo = lo + piece
-            if then is not None:
-                then()
             if n < NT - 1:
                 nc.sync.dma_start(out[n * P : (n + 1) * P, :], result[:])
 
@@ -170,13 +168,14 @@ def tile_list_tabgate_none_kernel(tc, tab_words, tab_scales, w4_words, w4_scales
         load_gates(1, 3)
         quantize_dw(1, 0, PAIR)
         for n in range(NT):
-            round_dw(0, n * P, (n + 1) * P, n % 3 == 0)
+            round_dw(0, n * P, (n + 1) * P, n % 3 == 0, "slot4" if n == NT - 1 else None)
         for n in range(NT):
             quantize_dw(0, n * P, (n + 1) * P)
         load_gates(2, 0)
+        load_gates(3, 4)
         open_tile(0)
         open_tile(1)
-        finish(0, [512, 512], lambda: load_gates(3, 1))
+        finish(0, [512, 512])
         finish(1, [1024])
         for n in range(2, NT):
             prepare_dw(1, n, False)

@@ -17,11 +17,17 @@ MULT = mybir.AluOpType.mult
 
 P = 128
 PACK = 4
-PASSES = K // (P * PACK)
-NT = M // P
+K_PASS = P * PACK
+PASSES = K // K_PASS
+ROW_TILES = M // P
 HALF = 512
 HALVES = S // HALF
-PAIR = 2 * P
+GROUP = 16
+SHIFT = 16
+EARLY_TILES = 2
+EARLY_COLS = EARLY_TILES * P
+GATE_PIECES = ([512, 512], [1024], [512, 512], [512, 384, 128])
+STORED_WHOLE = 2
 
 
 def tile_list_tabgate_none_kernel(tc, tab_words, tab_scales, w4_words, w4_scales, dw, gT, offs, out):
@@ -30,42 +36,42 @@ def tile_list_tabgate_none_kernel(tc, tab_words, tab_scales, w4_words, w4_scales
         keep = ctx.enter_context(tc.tile_pool(name="keep", bufs=1))
         psum = ctx.enter_context(tc.psum_pool(name="psum", bufs=1))
 
-        def tile(shape, dtype, name, tag=None):
-            return keep.tile(shape, dtype, name=name, tag=tag or name, align_bytes=64)
+        def tile(shape, dtype, name, slot=None):
+            return keep.tile(shape, dtype, name=name, tag=name if slot is None else "slot%d" % slot, align_bytes=64)
 
-        scale_window = tile([P, T], U8, "scale_window", "slot0")
+        scale_window = tile([P, T], U8, "scale_window", 0)
         nc.vector.memset(scale_window[:].bitcast(I32), 0)
         w4_planes = tile([P, PASSES, M], U8, "w4_planes")
         nc.vector.memset(w4_planes[:].rearrange("p a n -> p (a n)").bitcast(I32), 0)
-        tab_plane1 = tile([P, S], U8, "tab_plane1")
-        nc.vector.memset(tab_plane1[:].bitcast(I32), 0)
+        moved_plane = tile([P, S], U8, "moved_plane")
+        nc.vector.memset(moved_plane[:].bitcast(I32), 0)
 
-        offsets = keep.tile([P, S // 16], U16, name="offsets")
+        offsets = keep.tile([P, S // GROUP], U16, name="offsets")
         w4_codes = tile([P, PASSES, 2 * M], U8, "w4_codes")
-        word_window = [tile([P, T], U32, "word_window%d" % a, "slot%d" % (1 + a)) for a in range(PASSES)]
+        word_window = [tile([P, T], U32, "word_window%d" % a, 1 + a) for a in range(PASSES)]
         gate_window = {}
         dw_raw = {}
 
         def picks(lo, hi):
-            return offsets[:, lo // 16 : hi // 16]
+            return offsets[:, lo // GROUP : hi // GROUP]
 
         def load_words(a):
             nc.sync.dma_start(word_window[a][:].bitcast(I32), tab_words[a].rearrange("p t i -> p (t i)").bitcast(I32))
 
         def load_gates(n, slot):
-            gate_window[n] = tile([P, T], F32, "gate_window%d" % n, "slot%d" % slot)
+            gate_window[n] = tile([P, T], F32, "gate_window%d" % n, slot)
             nc.sync.dma_start(gate_window[n][:], gT[n * P : (n + 1) * P, :])
 
         def load_dw(a, lo, hi, slot):
-            raw = tile([P, PACK, hi - lo], F32, "dw_raw%d_%d" % (a, lo), "slot%d" % slot)
-            nc.sync.dma_start(raw[:], dw[a * 512 : (a + 1) * 512, lo:hi].rearrange("(p i) n -> p i n", i=PACK))
+            raw = tile([P, PACK, hi - lo], F32, "dw_raw%d_%d" % (a, lo), slot)
+            nc.sync.dma_start(raw[:], dw[a * K_PASS : (a + 1) * K_PASS, lo:hi].rearrange("(p i) n -> p i n", i=PACK))
             for n in range(lo // P, hi // P):
                 dw_raw[a, n] = (raw, lo)
 
         nc.sync.dma_start(offsets[:], offs)
         nc.sync.dma_start(w4_codes[:].bitcast(I32), w4_words.rearrange("a p w -> p a w").bitcast(I32))
         for r in range(4):
-            nc.sync.dma_start(scale_window[r:P:16, :].bitcast(I32), tab_scales[:, r:16:4, :].rearrange("a q t -> q a t").bitcast(I32))
+            nc.sync.dma_start(scale_window[r:P:SHIFT, :].bitcast(I32), tab_scales[:, r:16:4, :].rearrange("a q t -> q a t").bitcast(I32))
         load_words(0)
         load_words(1)
         for q in range(4):
@@ -73,9 +79,10 @@ def tile_list_tabgate_none_kernel(tc, tab_words, tab_scales, w4_words, w4_scales
                 w4_planes[32 * q : 32 * q + 4, :, :].bitcast(I32),
                 w4_scales[:, 4 * q : 4 * q + 4, :].rearrange("a r n -> r a n").bitcast(I32),
             )
-        load_dw(1, 0, PAIR, 3)
+        load_dw(1, 0, EARLY_COLS, 3)
 
-        tab_planes = tile([P, S], U8, "tab_planes")
+        gathered_scales = tile([P, S], U8, "gathered_scales")
+        tab_plane = [gathered_scales, moved_plane]
         tab_codes = [[tile([P, HALF], U32, "tab_codes%d_%d" % (a, h)) for h in range(HALVES)] for a in range(PASSES)]
 
         def gather_words(a, h):
@@ -83,103 +90,96 @@ def tile_list_tabgate_none_kernel(tc, tab_words, tab_scales, w4_words, w4_scales
 
         dw_codes = {}
         dw_planes = {}
-        dw_bf = {}
+        dw_rounded = {}
 
-        def round_dw(a, lo, hi, on_vector, tag=None):
-            g = tile([P, hi - lo, PACK], BF16, "dw_bf%d_%d" % (a, lo), tag)
-            dw_bf[a, lo] = g
-            dst = g[:].rearrange("p (c j) i -> p c i j", j=4)
+        def round_dw(a, lo, hi, copy, slot=None):
+            rounded = tile([P, hi - lo, PACK], BF16, "dw_rounded%d_%d" % (a, lo), slot)
+            dw_rounded[a, lo] = rounded
             raw, base = dw_raw[a, lo // P]
-            src = raw[:, :, lo - base : hi - base].rearrange("p i (c j) -> p c i j", j=4)
-            if on_vector:
-                nc.vector.tensor_copy(dst, src)
-            else:
-                nc.scalar.copy(dst, src)
+            copy(
+                rounded[:].rearrange("p (c j) i -> p c i j", j=4),
+                raw[:, :, lo - base : hi - base].rearrange("p i (c j) -> p c i j", j=4),
+            )
 
-        def quantize_dw(a, lo, hi, tag=None):
-            codes = tile([P, hi - lo], U32, "dw_codes%d_%d" % (a, lo), tag)
+        def quantize_dw(a, lo, hi):
+            codes = tile([P, hi - lo], U32, "dw_codes%d_%d" % (a, lo))
             plane = tile([P, hi - lo], U8, "dw_plane%d_%d" % (a, lo))
-            nc.vector.quantize_mx(out=codes[:].bitcast(FP8X4), scales=plane[:], in_=dw_bf[a, lo][:].rearrange("p c i -> p (c i)"))
+            nc.vector.quantize_mx(out=codes[:].bitcast(FP8X4), scales=plane[:], in_=dw_rounded[a, lo][:].rearrange("p c i -> p (c i)"))
             for n in range(lo // P, hi // P):
                 dw_codes[a, n] = codes[:, n * P - lo : (n + 1) * P - lo]
                 dw_planes[a, n] = plane[:, n * P - lo : (n + 1) * P - lo]
 
         acc = {}
 
+        def mx_pass(a, n, h, codes, plane, start, stop):
+            nc.tensor.matmul_mx(
+                out=acc[n][h][:],
+                lhsT=codes,
+                lhsT_scale=plane,
+                rhs=tab_codes[a][h][:].bitcast(FP8X4),
+                rhs_scale=tab_plane[a][:, h * HALF : (h + 1) * HALF],
+                start=start,
+                stop=stop,
+            )
+
+        def w4_pass(a, n, h):
+            codes = w4_codes[:, a, 2 * n * P : 2 * (n + 1) * P].bitcast(FP4X4)
+            mx_pass(a, n, h, codes, w4_planes[:, a, n * P : (n + 1) * P], a == 0, False)
+
+        def dw_pass(a, n, h, stop):
+            mx_pass(a, n, h, dw_codes[a, n].bitcast(FP8X4), dw_planes[a, n], False, stop)
+
         def open_tile(n):
-            acc[n] = [psum.tile([P, HALF], F32, name="acc%d_%d" % (n, h), tag="bank%d_%d" % (n % 2, h)) for h in range(HALVES)]
+            acc[n] = [psum.tile([P, HALF], F32, name="acc%d_%d" % (n, h), tag="bank%d_%d" % (n % EARLY_TILES, h)) for h in range(HALVES)]
             for h in range(HALVES):
-                w4_pass(0, n, h, True, False)
+                w4_pass(0, n, h)
 
-        def w4_pass(a, n, h, start, stop):
-            plane = tab_planes if a == 0 else tab_plane1
-            nc.tensor.matmul_mx(
-                out=acc[n][h][:],
-                lhsT=w4_codes[:, a, 2 * n * P : 2 * (n + 1) * P].bitcast(FP4X4),
-                lhsT_scale=w4_planes[:, a, n * P : (n + 1) * P],
-                rhs=tab_codes[a][h][:].bitcast(FP8X4),
-                rhs_scale=plane[:, h * HALF : (h + 1) * HALF],
-                start=start,
-                stop=stop,
-            )
-
-        def dw_pass(a, n, h, start, stop):
-            nc.tensor.matmul_mx(
-                out=acc[n][h][:],
-                lhsT=dw_codes[a, n].bitcast(FP8X4),
-                lhsT_scale=dw_planes[a, n],
-                rhs=tab_codes[a][h][:].bitcast(FP8X4),
-                rhs_scale=(tab_planes if a == 0 else tab_plane1)[:, h * HALF : (h + 1) * HALF],
-                start=start,
-                stop=stop,
-            )
-
-        def finish(n, pieces):
+        def close_tile(n):
+            last = 0 if n < EARLY_TILES else 1
             result = tile([P, S], F32, "result%d" % n)
             y = tile([P, S], F32, "y%d" % n)
             for h in range(HALVES):
-                w4_pass(1, n, h, False, False)
-                dw_pass(1 if n < 2 else 0, n, h, False, False)
-                dw_pass(0 if n < 2 else 1, n, h, False, True)
+                w4_pass(1, n, h)
+                dw_pass(1 - last, n, h, False)
+                dw_pass(last, n, h, True)
                 nc.scalar.copy(y[:, h * HALF : (h + 1) * HALF], acc[n][h][:])
             lo = 0
-            for piece in pieces:
-                nc.vector.tensor_tensor(result[:, lo : lo + piece], gate_window[n][:].indirect(picks(lo, lo + piece)), y[:, lo : lo + piece], MULT)
-                if n == NT - 1:
-                    nc.sync.dma_start(out[n * P : (n + 1) * P, lo : lo + piece], result[:, lo : lo + piece])
-                lo = lo + piece
-            if n < NT - 1:
+            for piece in GATE_PIECES[n]:
+                hi = lo + piece
+                nc.vector.tensor_tensor(result[:, lo:hi], gate_window[n][:].indirect(picks(lo, hi)), y[:, lo:hi], MULT)
+                if n >= STORED_WHOLE:
+                    nc.sync.dma_start(out[n * P : (n + 1) * P, lo:hi], result[:, lo:hi])
+                lo = hi
+            if n < STORED_WHOLE:
                 nc.sync.dma_start(out[n * P : (n + 1) * P, :], result[:])
 
-        def prepare_dw(a, n, on_vector):
-            round_dw(a, n * P, (n + 1) * P, on_vector)
-            quantize_dw(a, n * P, (n + 1) * P)
-
-        nc.vector.tensor_copy(tab_planes[:], scale_window[:].indirect(offsets[:]))
-        nc.sync.dma_start(tab_plane1[0:112, :].bitcast(I32), tab_planes[16:128, :].bitcast(I32))
+        nc.vector.tensor_copy(gathered_scales[:], scale_window[:].indirect(offsets[:]))
+        nc.sync.dma_start(moved_plane[0 : P - SHIFT, :].bitcast(I32), gathered_scales[SHIFT:P, :].bitcast(I32))
         load_dw(0, 0, M, 0)
         for h in range(HALVES):
             gather_words(0, h)
         load_gates(0, 1)
         for h in range(HALVES):
             gather_words(1, h)
-        load_dw(1, PAIR, M, 2)
-        round_dw(1, 0, PAIR, False)
+        load_dw(1, EARLY_COLS, M, 2)
+        round_dw(1, 0, EARLY_COLS, nc.scalar.copy)
         load_gates(1, 3)
-        quantize_dw(1, 0, PAIR)
-        for n in range(NT):
-            round_dw(0, n * P, (n + 1) * P, n % 3 == 0, "slot4" if n == NT - 1 else None)
-        for n in range(NT):
+        quantize_dw(1, 0, EARLY_COLS)
+        for n in range(ROW_TILES):
+            copy = nc.vector.tensor_copy if n in (0, ROW_TILES - 1) else nc.scalar.copy
+            round_dw(0, n * P, (n + 1) * P, copy, 4 if n == ROW_TILES - 1 else None)
+        for n in range(ROW_TILES):
             quantize_dw(0, n * P, (n + 1) * P)
         load_gates(2, 0)
         load_gates(3, 4)
-        open_tile(0)
-        open_tile(1)
-        finish(0, [512, 512])
-        finish(1, [1024])
-        for n in range(2, NT):
-            prepare_dw(1, n, False)
-        open_tile(2)
-        finish(2, [1024])
-        open_tile(3)
-        finish(3, [512, 256, 256])
+
+        for n in range(EARLY_TILES):
+            open_tile(n)
+        for n in range(EARLY_TILES):
+            close_tile(n)
+        for n in range(EARLY_TILES, ROW_TILES):
+            round_dw(1, n * P, (n + 1) * P, nc.scalar.copy)
+            quantize_dw(1, n * P, (n + 1) * P)
+        for n in range(EARLY_TILES, ROW_TILES):
+            open_tile(n)
+            close_tile(n)

@@ -23,66 +23,69 @@ ROW_TILES = M // P
 HALF = 512
 HALVES = S // HALF
 GROUP = 16
-SHIFT = 16
-EARLY_TILES = 2
-EARLY_COLS = EARLY_TILES * P
-GATE_PIECES = ([512, 512], [1024], [512, 512], [512, 384, 128])
-STORED_WHOLE = 2
+GATE_PIECES = ([256, 256, 512], [512, 512], [1024], [512, 384, 128])
+BANKS = 3
+STORED_WHOLE = 3
 
 
 def tile_list_tabgate_none_kernel(tc, tab_words, tab_scales, w4_words, w4_scales, dw, gT, offs, out):
     nc = tc.nc
     with ExitStack() as ctx:
         keep = ctx.enter_context(tc.tile_pool(name="keep", bufs=1))
+        placed = ctx.enter_context(tc.tile_pool(name="placed", bufs=1))
         psum = ctx.enter_context(tc.psum_pool(name="psum", bufs=1))
 
         def tile(shape, dtype, name, slot=None):
-            return keep.tile(shape, dtype, name=name, tag=name if slot is None else "slot%d" % slot, align_bytes=64)
+            if isinstance(slot, int):
+                return placed.tile(shape, dtype, name=name, offset=slot, align_bytes=64)
+            return keep.tile(shape, dtype, name=name, tag=name if slot is None else "slot_" + slot, align_bytes=64)
 
-        scale_window = tile([P, T], U8, "scale_window", 0)
+        scale_window = tile([P, T], U8, "scale_window", "a")
         nc.vector.memset(scale_window[:].bitcast(I32), 0)
         w4_planes = tile([P, PASSES, M], U8, "w4_planes")
         nc.vector.memset(w4_planes[:].rearrange("p a n -> p (a n)").bitcast(I32), 0)
-        moved_plane = tile([P, S], U8, "moved_plane")
-        nc.vector.memset(moved_plane[:].bitcast(I32), 0)
+        tab_planes = tile([P, PASSES, S], U8, "tab_planes")
+        nc.vector.memset(tab_planes[:].rearrange("p a n -> p (a n)").bitcast(I32), 0)
 
         offsets = keep.tile([P, S // GROUP], U16, name="offsets")
-        w4_codes = tile([P, PASSES, 2 * M], U8, "w4_codes")
-        word_window = [tile([P, T], U32, "word_window%d" % a, 1 + a) for a in range(PASSES)]
+        word_window = [tile([P, T], U32, "word_window%d" % a, (0, "c")[a]) for a in range(PASSES)]
         gate_window = {}
         dw_raw = {}
 
         def picks(lo, hi):
             return offsets[:, lo // GROUP : hi // GROUP]
 
-        def load_words(a):
-            nc.sync.dma_start(word_window[a][:].bitcast(I32), tab_words[a].rearrange("p t i -> p (t i)").bitcast(I32))
+        def load_words(a, lo=0, hi=T):
+            nc.sync.dma_start(word_window[a][:, lo:hi].bitcast(I32), tab_words[a].rearrange("p t i -> p (t i)").bitcast(I32)[:, lo:hi])
 
         def load_gates(n, slot):
             gate_window[n] = tile([P, T], F32, "gate_window%d" % n, slot)
             nc.sync.dma_start(gate_window[n][:], gT[n * P : (n + 1) * P, :])
 
-        def load_dw(a, lo, hi, slot):
-            raw = tile([P, PACK, hi - lo], F32, "dw_raw%d_%d" % (a, lo), slot)
-            nc.sync.dma_start(raw[:], dw[a * K_PASS : (a + 1) * K_PASS, lo:hi].rearrange("(p i) n -> p i n", i=PACK))
-            for n in range(lo // P, hi // P):
-                dw_raw[a, n] = (raw, lo)
+        def load_dw(a, slot):
+            dw_raw[a] = tile([P, PACK, M], F32, "dw_raw%d" % a, slot)
+            nc.sync.dma_start(dw_raw[a][:], dw[a * K_PASS : (a + 1) * K_PASS, :].rearrange("(p i) n -> p i n", i=PACK))
+
+        w4_codes = [tile([P, 2 * M], U8, "w4_codes%d" % a, (None, 0)[a]) for a in range(PASSES)]
+
+        def load_w4(a):
+            nc.sync.dma_start(w4_codes[a][:].bitcast(I32), w4_words[a].bitcast(I32))
 
         nc.sync.dma_start(offsets[:], offs)
-        nc.sync.dma_start(w4_codes[:].bitcast(I32), w4_words.rearrange("a p w -> p a w").bitcast(I32))
-        for r in range(4):
-            nc.sync.dma_start(scale_window[r:P:SHIFT, :].bitcast(I32), tab_scales[:, r:16:4, :].rearrange("a q t -> q a t").bitcast(I32))
-        load_words(0)
+        load_words(0, 0, T // 2)
+        for a in range(PASSES):
+            nc.sync.dma_start(scale_window[4 * a : P : 8, :].bitcast(I32), tab_scales[a].bitcast(I32))
+        load_words(0, T // 2, T)
         load_words(1)
+        load_w4(0)
         for q in range(4):
             nc.sync.dma_start(
                 w4_planes[32 * q : 32 * q + 4, :, :].bitcast(I32),
                 w4_scales[:, 4 * q : 4 * q + 4, :].rearrange("a r n -> r a n").bitcast(I32),
             )
-        load_dw(1, 0, EARLY_COLS, 3)
+        load_dw(0, "d")
 
         gathered_scales = tile([P, S], U8, "gathered_scales")
-        tab_plane = [gathered_scales, moved_plane]
         tab_codes = [[tile([P, HALF], U32, "tab_codes%d_%d" % (a, h)) for h in range(HALVES)] for a in range(PASSES)]
 
         def gather_words(a, h):
@@ -92,57 +95,89 @@ def tile_list_tabgate_none_kernel(tc, tab_words, tab_scales, w4_words, w4_scales
         dw_planes = {}
         dw_rounded = {}
 
-        def round_dw(a, lo, hi, copy, slot=None):
-            rounded = tile([P, hi - lo, PACK], BF16, "dw_rounded%d_%d" % (a, lo), slot)
-            dw_rounded[a, lo] = rounded
-            raw, base = dw_raw[a, lo // P]
+        def round_dw(a, n, copy, slot=None):
+            dw_rounded[a, n] = tile([P, P, PACK], BF16, "dw_rounded%d_%d" % (a, n), slot)
             copy(
-                rounded[:].rearrange("p (c j) i -> p c i j", j=4),
-                raw[:, :, lo - base : hi - base].rearrange("p i (c j) -> p c i j", j=4),
+                dw_rounded[a, n][:].rearrange("p (c j) i -> p c i j", j=4),
+                dw_raw[a][:, :, n * P : (n + 1) * P].rearrange("p i (c j) -> p c i j", j=4),
             )
 
-        def quantize_dw(a, lo, hi):
-            codes = tile([P, hi - lo], U32, "dw_codes%d_%d" % (a, lo))
-            plane = tile([P, hi - lo], U8, "dw_plane%d_%d" % (a, lo))
-            nc.vector.quantize_mx(out=codes[:].bitcast(FP8X4), scales=plane[:], in_=dw_rounded[a, lo][:].rearrange("p c i -> p (c i)"))
-            for n in range(lo // P, hi // P):
-                dw_codes[a, n] = codes[:, n * P - lo : (n + 1) * P - lo]
-                dw_planes[a, n] = plane[:, n * P - lo : (n + 1) * P - lo]
+        def quantize_dw(a, n):
+            dw_codes[a, n] = tile([P, P], U32, "dw_codes%d_%d" % (a, n))
+            dw_planes[a, n] = tile([P, P], U8, "dw_plane%d_%d" % (a, n))
+            nc.vector.quantize_mx(
+                out=dw_codes[a, n][:].bitcast(FP8X4), scales=dw_planes[a, n][:], in_=dw_rounded[a, n][:].rearrange("p c i -> p (c i)")
+            )
 
         acc = {}
 
         def mx_pass(a, n, h, codes, plane, start, stop):
             nc.tensor.matmul_mx(
-                out=acc[n][h][:],
+                out=acc[n, h][:],
                 lhsT=codes,
                 lhsT_scale=plane,
                 rhs=tab_codes[a][h][:].bitcast(FP8X4),
-                rhs_scale=tab_plane[a][:, h * HALF : (h + 1) * HALF],
+                rhs_scale=tab_planes[:, a, h * HALF : (h + 1) * HALF],
                 start=start,
                 stop=stop,
             )
 
         def w4_pass(a, n, h):
-            codes = w4_codes[:, a, 2 * n * P : 2 * (n + 1) * P].bitcast(FP4X4)
+            codes = w4_codes[a][:, 2 * n * P : 2 * (n + 1) * P].bitcast(FP4X4)
             mx_pass(a, n, h, codes, w4_planes[:, a, n * P : (n + 1) * P], a == 0, False)
 
-        def dw_pass(a, n, h, stop):
-            mx_pass(a, n, h, dw_codes[a, n].bitcast(FP8X4), dw_planes[a, n], False, stop)
+        def dw_pass(a, n, h):
+            mx_pass(a, n, h, dw_codes[a, n][:].bitcast(FP8X4), dw_planes[a, n][:], False, a == PASSES - 1)
 
-        def open_tile(n):
-            acc[n] = [psum.tile([P, HALF], F32, name="acc%d_%d" % (n, h), tag="bank%d_%d" % (n % EARLY_TILES, h)) for h in range(HALVES)]
-            for h in range(HALVES):
-                w4_pass(0, n, h)
+        nc.vector.tensor_copy(gathered_scales[:], scale_window[:].indirect(offsets[:]))
+        for q in range(4):
+            nc.sync.dma_start(
+                tab_planes[32 * q : 32 * q + 4, :, :].bitcast(I32),
+                gathered_scales[32 * q : 32 * q + 32 : 4, :].bitcast(I32),
+            )
+        load_dw(1, "a")
+        for h in range(HALVES):
+            gather_words(0, h)
+        load_w4(1)
+        load_gates(0, 2 * M)
+        for h in range(HALVES):
+            gather_words(1, h)
+        load_gates(1, "c")
+        for n in (0, 2, 3, 1):
+            round_dw(0, n, nc.scalar.copy, "e" if n == 0 else None)
+            quantize_dw(0, n)
+        load_gates(2, "e")
+        load_gates(3, "d")
+        round_dw(1, 0, nc.vector.tensor_copy)
+        quantize_dw(1, 0)
+        round_dw(1, 1, nc.scalar.copy)
+        round_dw(1, 2, nc.vector.tensor_copy)
+        round_dw(1, 3, nc.vector.tensor_copy)
+        for n in range(1, ROW_TILES):
+            quantize_dw(1, n)
 
-        def close_tile(n):
-            last = 0 if n < EARLY_TILES else 1
+        def open_sum(n, h):
+            acc[n, h] = psum.tile([P, HALF], F32, name="acc%d_%d" % (n, h), tag="bank%d" % ((n * HALVES + h) % BANKS))
+            w4_pass(0, n, h)
+
+        for b in range(BANKS):
+            open_sum(*divmod(b, HALVES))
+        for h in range(HALVES):
+            dw_pass(0, 0, h)
+            w4_pass(1, 0, h)
+        for n in range(ROW_TILES):
             result = tile([P, S], F32, "result%d" % n)
             y = tile([P, S], F32, "y%d" % n)
             for h in range(HALVES):
-                w4_pass(1, n, h)
-                dw_pass(1 - last, n, h, False)
-                dw_pass(last, n, h, True)
-                nc.scalar.copy(y[:, h * HALF : (h + 1) * HALF], acc[n][h][:])
+                if (n, h) not in acc:
+                    open_sum(n, h)
+                if n > 0:
+                    dw_pass(0, n, h)
+                    w4_pass(1, n, h)
+                dw_pass(1, n, h)
+                step = HALF // 2 if (n, h) == (0, 0) else HALF
+                for lo in range(0, HALF, step):
+                    nc.scalar.copy(y[:, h * HALF + lo : h * HALF + lo + step], acc[n, h][:, lo : lo + step])
             lo = 0
             for piece in GATE_PIECES[n]:
                 hi = lo + piece
@@ -152,34 +187,3 @@ def tile_list_tabgate_none_kernel(tc, tab_words, tab_scales, w4_words, w4_scales
                 lo = hi
             if n < STORED_WHOLE:
                 nc.sync.dma_start(out[n * P : (n + 1) * P, :], result[:])
-
-        nc.vector.tensor_copy(gathered_scales[:], scale_window[:].indirect(offsets[:]))
-        nc.sync.dma_start(moved_plane[0 : P - SHIFT, :].bitcast(I32), gathered_scales[SHIFT:P, :].bitcast(I32))
-        load_dw(0, 0, M, 0)
-        for h in range(HALVES):
-            gather_words(0, h)
-        load_gates(0, 1)
-        for h in range(HALVES):
-            gather_words(1, h)
-        load_dw(1, EARLY_COLS, M, 2)
-        round_dw(1, 0, EARLY_COLS, nc.scalar.copy)
-        load_gates(1, 3)
-        quantize_dw(1, 0, EARLY_COLS)
-        for n in range(ROW_TILES):
-            copy = nc.vector.tensor_copy if n in (0, ROW_TILES - 1) else nc.scalar.copy
-            round_dw(0, n * P, (n + 1) * P, copy, 4 if n == ROW_TILES - 1 else None)
-        for n in range(ROW_TILES):
-            quantize_dw(0, n * P, (n + 1) * P)
-        load_gates(2, 0)
-        load_gates(3, 4)
-
-        for n in range(EARLY_TILES):
-            open_tile(n)
-        for n in range(EARLY_TILES):
-            close_tile(n)
-        for n in range(EARLY_TILES, ROW_TILES):
-            round_dw(1, n * P, (n + 1) * P, nc.scalar.copy)
-            quantize_dw(1, n * P, (n + 1) * P)
-        for n in range(EARLY_TILES, ROW_TILES):
-            open_tile(n)
-            close_tile(n)

@@ -1,4 +1,5 @@
 from contextlib import ExitStack
+from itertools import accumulate
 
 import concourse.mybir as mybir
 
@@ -23,8 +24,9 @@ ROW_TILES = M // P
 HALF = 512
 HALVES = S // HALF
 GROUP = 16
-GATE_PIECES = ([256, 256, 512], [512, 512], [1024], [512, 384, 128])
-BANKS = 3
+GATE_PIECES = ([256, 256, 256, 256], [512, 512], [1024], [512, 384, 128])
+SUM_PIECES = ([256, 256, 256, 256], [512, 512], [512, 512], [512, 512])
+BANKS = 8
 STORED_WHOLE = 3
 
 
@@ -44,11 +46,11 @@ def tile_list_tabgate_none_kernel(tc, tab_words, tab_scales, w4_words, w4_scales
         nc.vector.memset(scale_window[:].bitcast(I32), 0)
         w4_planes = tile([P, PASSES, M], U8, "w4_planes")
         nc.vector.memset(w4_planes[:].rearrange("p a n -> p (a n)").bitcast(I32), 0)
-        tab_planes = tile([P, PASSES, S], U8, "tab_planes")
-        nc.vector.memset(tab_planes[:].rearrange("p a n -> p (a n)").bitcast(I32), 0)
+        moved_plane = tile([P, S], U8, "moved_plane")
+        nc.vector.memset(moved_plane[:].bitcast(I32), 0)
 
         offsets = keep.tile([P, S // GROUP], U16, name="offsets")
-        word_window = [tile([P, T], U32, "word_window%d" % a, (0, "c")[a]) for a in range(PASSES)]
+        word_window = [tile([P, T], U32, "word_window%d" % a, (0, "a")[a]) for a in range(PASSES)]
         gate_window = {}
         dw_raw = {}
 
@@ -73,23 +75,25 @@ def tile_list_tabgate_none_kernel(tc, tab_words, tab_scales, w4_words, w4_scales
 
         nc.sync.dma_start(offsets[:], offs)
         load_words(0, 0, T // 2)
-        for a in range(PASSES):
-            nc.sync.dma_start(scale_window[4 * a : P : 8, :].bitcast(I32), tab_scales[a].bitcast(I32))
+        for q in range(4):
+            nc.sync.dma_start(scale_window[32 * q : 32 * q + 4, :].bitcast(I32), tab_scales[0, 4 * q : 4 * q + 4, :].bitcast(I32))
+        nc.sync.dma_start(scale_window[4:P:8, :].bitcast(I32), tab_scales[1].bitcast(I32))
         load_words(0, T // 2, T)
-        load_words(1)
+        load_dw(0, "d")
         load_w4(0)
         for q in range(4):
             nc.sync.dma_start(
                 w4_planes[32 * q : 32 * q + 4, :, :].bitcast(I32),
                 w4_scales[:, 4 * q : 4 * q + 4, :].rearrange("a r n -> r a n").bitcast(I32),
             )
-        load_dw(0, "d")
+        load_dw(1, "c")
 
         gathered_scales = tile([P, S], U8, "gathered_scales")
-        tab_codes = [[tile([P, HALF], U32, "tab_codes%d_%d" % (a, h)) for h in range(HALVES)] for a in range(PASSES)]
+        tab_plane = [gathered_scales, moved_plane]
+        tab_codes = [tile([P, S], U32, "tab_codes%d" % a) for a in range(PASSES)]
 
-        def gather_words(a, h):
-            nc.vector.tensor_copy(tab_codes[a][h][:], word_window[a][:].indirect(picks(h * HALF, (h + 1) * HALF)))
+        def gather_words(a, lo, hi):
+            nc.vector.tensor_copy(tab_codes[a][:, lo:hi], word_window[a][:].indirect(picks(lo, hi)))
 
         dw_codes = {}
         dw_planes = {}
@@ -109,81 +113,70 @@ def tile_list_tabgate_none_kernel(tc, tab_words, tab_scales, w4_words, w4_scales
                 out=dw_codes[a, n][:].bitcast(FP8X4), scales=dw_planes[a, n][:], in_=dw_rounded[a, n][:].rearrange("p c i -> p (c i)")
             )
 
-        acc = {}
-
-        def mx_pass(a, n, h, codes, plane, start, stop):
+        def mx_pass(acc, a, lo, hi, codes, plane, start, stop):
             nc.tensor.matmul_mx(
-                out=acc[n, h][:],
+                out=acc,
                 lhsT=codes,
                 lhsT_scale=plane,
-                rhs=tab_codes[a][h][:].bitcast(FP8X4),
-                rhs_scale=tab_planes[:, a, h * HALF : (h + 1) * HALF],
+                rhs=tab_codes[a][:, lo:hi].bitcast(FP8X4),
+                rhs_scale=tab_plane[a][:, lo:hi],
                 start=start,
                 stop=stop,
             )
 
-        def w4_pass(a, n, h):
-            codes = w4_codes[a][:, 2 * n * P : 2 * (n + 1) * P].bitcast(FP4X4)
-            mx_pass(a, n, h, codes, w4_planes[:, a, n * P : (n + 1) * P], a == 0, False)
+        acc = {}
 
-        def dw_pass(a, n, h):
-            mx_pass(a, n, h, dw_codes[a, n][:].bitcast(FP8X4), dw_planes[a, n][:], False, a == PASSES - 1)
+        def passes(a, n, lo, hi):
+            if a == 0:
+                acc[n, lo] = psum.tile([P, hi - lo], F32, name="acc%d_%d" % (n, lo), tag="bank%d" % (len(acc) % BANKS))
+            codes = w4_codes[a][:, 2 * n * P : 2 * (n + 1) * P].bitcast(FP4X4)
+            step = HALF if hi - lo == HALF else P
+            for j in range(lo, hi, step):
+                mx_pass(acc[n, lo][:, j - lo : j - lo + step], a, j, j + step, codes, w4_planes[:, a, n * P : (n + 1) * P], a == 0 and j == lo, False)
+            mx_pass(acc[n, lo][:], a, lo, hi, dw_codes[a, n][:].bitcast(FP8X4), dw_planes[a, n][:], False, a == 1)
+
+        def ranges(pieces):
+            ends = list(accumulate(pieces))
+            return list(zip([0] + ends, ends))
 
         nc.vector.tensor_copy(gathered_scales[:], scale_window[:].indirect(offsets[:]))
         for q in range(4):
             nc.sync.dma_start(
-                tab_planes[32 * q : 32 * q + 4, :, :].bitcast(I32),
-                gathered_scales[32 * q : 32 * q + 32 : 4, :].bitcast(I32),
+                moved_plane[32 * q : 32 * q + 4, :].bitcast(I32),
+                gathered_scales[32 * q + 4 : 32 * q + 32 : 8, :].bitcast(I32),
             )
-        load_dw(1, "a")
+        load_words(1)
         for h in range(HALVES):
-            gather_words(0, h)
+            gather_words(0, h * HALF, (h + 1) * HALF)
         load_w4(1)
         load_gates(0, 2 * M)
-        for h in range(HALVES):
-            gather_words(1, h)
-        load_gates(1, "c")
-        for n in (0, 2, 3, 1):
-            round_dw(0, n, nc.scalar.copy, "e" if n == 0 else None)
+        for n in range(ROW_TILES):
+            round_dw(0, n, nc.scalar.copy)
             quantize_dw(0, n)
-        load_gates(2, "e")
-        load_gates(3, "d")
-        round_dw(1, 0, nc.vector.tensor_copy)
-        quantize_dw(1, 0)
-        round_dw(1, 1, nc.scalar.copy)
-        round_dw(1, 2, nc.vector.tensor_copy)
-        round_dw(1, 3, nc.vector.tensor_copy)
-        for n in range(1, ROW_TILES):
+        load_gates(1, "d")
+        for n in range(ROW_TILES):
+            round_dw(1, n, nc.scalar.copy if n % 2 else nc.vector.tensor_copy)
+        for n in range(ROW_TILES):
             quantize_dw(1, n)
+        load_gates(2, "c")
+        for lo, hi in ranges(SUM_PIECES[0]):
+            gather_words(1, lo, hi)
+        load_gates(3, "a")
 
-        def open_sum(n, h):
-            acc[n, h] = psum.tile([P, HALF], F32, name="acc%d_%d" % (n, h), tag="bank%d" % ((n * HALVES + h) % BANKS))
-            w4_pass(0, n, h)
-
-        for b in range(BANKS):
-            open_sum(*divmod(b, HALVES))
-        for h in range(HALVES):
-            dw_pass(0, 0, h)
-            w4_pass(1, 0, h)
+        sums = [(n, lo, hi) for n in range(ROW_TILES) for lo, hi in ranges(SUM_PIECES[n])]
+        for n, lo, hi in sums[:BANKS]:
+            passes(0, n, lo, hi)
         for n in range(ROW_TILES):
             result = tile([P, S], F32, "result%d" % n)
             y = tile([P, S], F32, "y%d" % n)
-            for h in range(HALVES):
-                if (n, h) not in acc:
-                    open_sum(n, h)
-                if n > 0:
-                    dw_pass(0, n, h)
-                    w4_pass(1, n, h)
-                dw_pass(1, n, h)
-                step = HALF // 2 if (n, h) == (0, 0) else HALF
-                for lo in range(0, HALF, step):
-                    nc.scalar.copy(y[:, h * HALF + lo : h * HALF + lo + step], acc[n, h][:, lo : lo + step])
-            lo = 0
-            for piece in GATE_PIECES[n]:
-                hi = lo + piece
+            for lo, hi in ranges(SUM_PIECES[n]):
+                if (n, lo) not in acc:
+                    passes(0, n, lo, hi)
+                passes(1, n, lo, hi)
+                nc.scalar.copy(y[:, lo:hi], acc[n, lo][:])
+            for lo, hi in ranges(GATE_PIECES[n]):
                 nc.vector.tensor_tensor(result[:, lo:hi], gate_window[n][:].indirect(picks(lo, hi)), y[:, lo:hi], MULT)
                 if n >= STORED_WHOLE:
                     nc.sync.dma_start(out[n * P : (n + 1) * P, lo:hi], result[:, lo:hi])
-                lo = hi
             if n < STORED_WHOLE:
                 nc.sync.dma_start(out[n * P : (n + 1) * P, :], result[:])

@@ -24,7 +24,7 @@ ROW_TILES = M // P
 HALF = 512
 HALVES = S // HALF
 GROUP = 16
-GATE_PIECES = ([256, 256, 256, 256], [512, 512], [1024], [512, 384, 128])
+GATE_PIECES = ([256, 256, 256, 256], [512, 512], [512, 512], [512, 384, 128])
 SUM_PIECES = ([256, 256, 256, 256], [512, 512], [512, 512], [512, 512])
 BANKS = 8
 STORED_WHOLE = 3
@@ -68,10 +68,15 @@ def tile_list_tabgate_none_kernel(tc, tab_words, tab_scales, w4_words, w4_scales
             dw_raw[a] = tile([P, PACK, M], F32, "dw_raw%d" % a, slot)
             nc.sync.dma_start(dw_raw[a][:], dw[a * K_PASS : (a + 1) * K_PASS, :].rearrange("(p i) n -> p i n", i=PACK))
 
-        w4_codes = [tile([P, 2 * M], U8, "w4_codes%d" % a, (None, 0)[a]) for a in range(PASSES)]
+        w4_codes = {}
 
-        def load_w4(a):
-            nc.sync.dma_start(w4_codes[a][:].bitcast(I32), w4_words[a].bitcast(I32))
+        def load_w4(first, last):
+            lo, hi = 2 * P * first, 2 * P * last
+            words = tile([P, PASSES, hi - lo], U8, "w4_codes%d" % first, PASSES * lo)
+            nc.sync.dma_start(words[:].bitcast(I32), w4_words[:, :, lo:hi].rearrange("a p w -> p a w").bitcast(I32))
+            for n in range(first, last):
+                for a in range(PASSES):
+                    w4_codes[a, n] = words[:, a, 2 * P * (n - first) : 2 * P * (n - first + 1)]
 
         nc.sync.dma_start(offsets[:], offs)
         load_words(0, 0, T // 2)
@@ -80,7 +85,6 @@ def tile_list_tabgate_none_kernel(tc, tab_words, tab_scales, w4_words, w4_scales
         nc.sync.dma_start(scale_window[4:P:8, :].bitcast(I32), tab_scales[1].bitcast(I32))
         load_words(0, T // 2, T)
         load_dw(0, "d")
-        load_w4(0)
         for q in range(4):
             nc.sync.dma_start(
                 w4_planes[32 * q : 32 * q + 4, :, :].bitcast(I32),
@@ -126,14 +130,18 @@ def tile_list_tabgate_none_kernel(tc, tab_words, tab_scales, w4_words, w4_scales
 
         acc = {}
 
-        def passes(a, n, lo, hi):
+        def dw_pass(a, n, lo, hi, stop=False):
             if a == 0:
                 acc[n, lo] = psum.tile([P, hi - lo], F32, name="acc%d_%d" % (n, lo), tag="bank%d" % (len(acc) % BANKS))
-            codes = w4_codes[a][:, 2 * n * P : 2 * (n + 1) * P].bitcast(FP4X4)
+            mx_pass(acc[n, lo][:], a, lo, hi, dw_codes[a, n][:].bitcast(FP8X4), dw_planes[a, n][:], a == 0, stop)
+
+        def w4_pass(a, n, lo, hi, stop=False):
             step = HALF if hi - lo == HALF else P
             for j in range(lo, hi, step):
-                mx_pass(acc[n, lo][:, j - lo : j - lo + step], a, j, j + step, codes, w4_planes[:, a, n * P : (n + 1) * P], a == 0 and j == lo, False)
-            mx_pass(acc[n, lo][:], a, lo, hi, dw_codes[a, n][:].bitcast(FP8X4), dw_planes[a, n][:], False, a == 1)
+                mx_pass(
+                    acc[n, lo][:, j - lo : j - lo + step], a, j, j + step,
+                    w4_codes[a, n].bitcast(FP4X4), w4_planes[:, a, n * P : (n + 1) * P], False, stop and j + step == hi,
+                )
 
         def ranges(pieces):
             ends = list(accumulate(pieces))
@@ -148,8 +156,9 @@ def tile_list_tabgate_none_kernel(tc, tab_words, tab_scales, w4_words, w4_scales
         load_words(1)
         for h in range(HALVES):
             gather_words(0, h * HALF, (h + 1) * HALF)
-        load_w4(1)
-        load_gates(0, 2 * M)
+        load_w4(0, 2)
+        load_gates(0, PASSES * 2 * M)
+        load_w4(2, ROW_TILES)
         for n in range(ROW_TILES):
             round_dw(0, n, nc.scalar.copy)
             quantize_dw(0, n)
@@ -165,14 +174,19 @@ def tile_list_tabgate_none_kernel(tc, tab_words, tab_scales, w4_words, w4_scales
 
         sums = [(n, lo, hi) for n in range(ROW_TILES) for lo, hi in ranges(SUM_PIECES[n])]
         for n, lo, hi in sums[:BANKS]:
-            passes(0, n, lo, hi)
+            dw_pass(0, n, lo, hi)
+        for lo, hi in ranges(SUM_PIECES[0]):
+            w4_pass(0, 0, lo, hi)
         for n in range(ROW_TILES):
             result = tile([P, S], F32, "result%d" % n)
             y = tile([P, S], F32, "y%d" % n)
             for lo, hi in ranges(SUM_PIECES[n]):
                 if (n, lo) not in acc:
-                    passes(0, n, lo, hi)
-                passes(1, n, lo, hi)
+                    dw_pass(0, n, lo, hi)
+                if n > 0:
+                    w4_pass(0, n, lo, hi)
+                w4_pass(1, n, lo, hi)
+                dw_pass(1, n, lo, hi, True)
                 nc.scalar.copy(y[:, lo:hi], acc[n, lo][:])
             for lo, hi in ranges(GATE_PIECES[n]):
                 nc.vector.tensor_tensor(result[:, lo:hi], gate_window[n][:].indirect(picks(lo, hi)), y[:, lo:hi], MULT)

@@ -26,7 +26,7 @@ HALVES = S // HALF
 GROUP = 16
 GATE_PIECES = ([256, 256, 256, 256], [512, 512], [512, 512], [512, 384, 128])
 SUM_PIECES = ([256, 256, 256, 256], [512, 512], [512, 512], [512, 512])
-BANKS = 8
+BANKS = 7
 STORED_WHOLE = 3
 
 
@@ -50,7 +50,7 @@ def tile_list_tabgate_none_kernel(tc, tab_words, tab_scales, w4_words, w4_scales
         nc.vector.memset(moved_plane[:].bitcast(I32), 0)
 
         offsets = keep.tile([P, S // GROUP], U16, name="offsets")
-        word_window = [tile([P, T], U32, "word_window%d" % a, (0, "a")[a]) for a in range(PASSES)]
+        word_window = [tile([P, T], U32, "word_window%d" % a, (0, "b")[a]) for a in range(PASSES)]
         gate_window = {}
         dw_raw = {}
 
@@ -91,6 +91,7 @@ def tile_list_tabgate_none_kernel(tc, tab_words, tab_scales, w4_words, w4_scales
                 w4_scales[:, 4 * q : 4 * q + 4, :].rearrange("a r n -> r a n").bitcast(I32),
             )
         load_dw(1, "c")
+        load_words(1)
 
         gathered_scales = tile([P, S], U8, "gathered_scales")
         tab_plane = [gathered_scales, moved_plane]
@@ -153,14 +154,13 @@ def tile_list_tabgate_none_kernel(tc, tab_words, tab_scales, w4_words, w4_scales
                 moved_plane[32 * q : 32 * q + 4, :].bitcast(I32),
                 gathered_scales[32 * q + 4 : 32 * q + 32 : 8, :].bitcast(I32),
             )
-        load_words(1)
         for h in range(HALVES):
             gather_words(0, h * HALF, (h + 1) * HALF)
         load_w4(0, 2)
         load_gates(0, PASSES * 2 * M)
         load_w4(2, ROW_TILES)
         for n in range(ROW_TILES):
-            round_dw(0, n, nc.scalar.copy)
+            round_dw(0, n, nc.scalar.copy if n < ROW_TILES - 1 else nc.vector.tensor_copy, "e" if n % 2 else None)
             quantize_dw(0, n)
         load_gates(1, "d")
         for n in range(ROW_TILES):
@@ -170,26 +170,40 @@ def tile_list_tabgate_none_kernel(tc, tab_words, tab_scales, w4_words, w4_scales
         load_gates(2, "c")
         for lo, hi in ranges(SUM_PIECES[0]):
             gather_words(1, lo, hi)
-        load_gates(3, "a")
+        load_gates(3, "b")
 
         sums = [(n, lo, hi) for n in range(ROW_TILES) for lo, hi in ranges(SUM_PIECES[n])]
         for n, lo, hi in sums[:BANKS]:
             dw_pass(0, n, lo, hi)
+        ys = [tile([P, S], F32, "y%d" % n) for n in range(ROW_TILES)]
+
+        def close(n, lo, hi):
+            w4_pass(1, n, lo, hi)
+            dw_pass(1, n, lo, hi, True)
+
+        def copy_out(n, lo, hi):
+            nc.scalar.copy(ys[n][:, lo:hi], acc[n, lo][:])
+
         for lo, hi in ranges(SUM_PIECES[0]):
             w4_pass(0, 0, lo, hi)
+            close(0, lo, hi)
+            half = lo // HALF * HALF
+            if lo == half:
+                w4_pass(0, 1, half, half + HALF)
+            else:
+                close(1, half, half + HALF)
+            copy_out(0, lo, hi)
+        for n, lo, hi in sums[len(SUM_PIECES[0]) :]:
+            if (n, lo) not in acc:
+                dw_pass(0, n, lo, hi)
+            if n > 1:
+                w4_pass(0, n, lo, hi)
+                close(n, lo, hi)
+            copy_out(n, lo, hi)
         for n in range(ROW_TILES):
             result = tile([P, S], F32, "result%d" % n)
-            y = tile([P, S], F32, "y%d" % n)
-            for lo, hi in ranges(SUM_PIECES[n]):
-                if (n, lo) not in acc:
-                    dw_pass(0, n, lo, hi)
-                if n > 0:
-                    w4_pass(0, n, lo, hi)
-                w4_pass(1, n, lo, hi)
-                dw_pass(1, n, lo, hi, True)
-                nc.scalar.copy(y[:, lo:hi], acc[n, lo][:])
             for lo, hi in ranges(GATE_PIECES[n]):
-                nc.vector.tensor_tensor(result[:, lo:hi], gate_window[n][:].indirect(picks(lo, hi)), y[:, lo:hi], MULT)
+                nc.vector.tensor_tensor(result[:, lo:hi], gate_window[n][:].indirect(picks(lo, hi)), ys[n][:, lo:hi], MULT)
                 if n >= STORED_WHOLE:
                     nc.sync.dma_start(out[n * P : (n + 1) * P, lo:hi], result[:, lo:hi])
             if n < STORED_WHOLE:

@@ -26,7 +26,7 @@ HALVES = S // HALF
 GROUP = 16
 GATE_PIECES = ([256, 256, 256, 256], [512, 512], [512, 512], [512, 384, 128])
 SUM_PIECES = ([256, 256, 256, 256], [512, 512], [512, 512], [512, 512])
-BANKS = 7
+BANKS = 8
 STORED_WHOLE = 3
 
 
@@ -72,7 +72,7 @@ def tile_list_tabgate_none_kernel(tc, tab_words, tab_scales, w4_words, w4_scales
 
         def load_w4(first, last):
             lo, hi = 2 * P * first, 2 * P * last
-            words = tile([P, PASSES, hi - lo], U8, "w4_codes%d" % first, PASSES * lo)
+            words = tile([P, PASSES, hi - lo], U8, "w4_codes%d" % first, "e" if first else 0)
             nc.sync.dma_start(words[:].bitcast(I32), w4_words[:, :, lo:hi].rearrange("a p w -> p a w").bitcast(I32))
             for n in range(first, last):
                 for a in range(PASSES):
@@ -158,11 +158,11 @@ def tile_list_tabgate_none_kernel(tc, tab_words, tab_scales, w4_words, w4_scales
             gather_words(0, h * HALF, (h + 1) * HALF)
         load_w4(0, 2)
         load_gates(0, PASSES * 2 * M)
-        load_w4(2, ROW_TILES)
         for n in range(ROW_TILES):
             round_dw(0, n, nc.scalar.copy if n < ROW_TILES - 1 else nc.vector.tensor_copy, "e" if n % 2 else None)
             quantize_dw(0, n)
         load_gates(1, "d")
+        load_w4(2, ROW_TILES)
         for n in range(ROW_TILES):
             round_dw(1, n, nc.scalar.copy if n % 2 else nc.vector.tensor_copy)
         for n in range(ROW_TILES):

@@ -24,9 +24,11 @@ ROW_TILES = M // P
 HALF = 512
 HALVES = S // HALF
 GROUP = 16
-GATE_PIECES = ([256, 256, 256, 256], [512, 512], [512, 512], [512, 384, 128])
-SUM_PIECES = ([256, 256, 256, 256], [512, 512], [512, 512], [512, 512])
-BANKS = 8
+QUAD = 32
+WINDOW = 4 * T
+GATE_PIECES = ([256, 256, 512], [1024], [1024], [512, 384, 128])
+COPY_PIECES = ([256, 256, 512], [512, 512], [512, 512], [512, 512])
+EARLY_TILES = 2
 STORED_WHOLE = 3
 
 
@@ -39,26 +41,29 @@ def tile_list_tabgate_none_kernel(tc, tab_words, tab_scales, w4_words, w4_scales
 
         def tile(shape, dtype, name, slot=None):
             if isinstance(slot, int):
-                return placed.tile(shape, dtype, name=name, offset=slot, align_bytes=64)
-            return keep.tile(shape, dtype, name=name, tag=name if slot is None else "slot_" + slot, align_bytes=64)
+                return placed.tile(shape, dtype, name=name, offset=slot, align_bytes=256)
+            return keep.tile(shape, dtype, name=name, tag=name if slot is None else "slot_" + slot, align_bytes=256)
 
-        scale_window = tile([P, T], U8, "scale_window", "a")
-        nc.vector.memset(scale_window[:].bitcast(I32), 0)
         w4_planes = tile([P, PASSES, M], U8, "w4_planes")
         nc.vector.memset(w4_planes[:].rearrange("p a n -> p (a n)").bitcast(I32), 0)
-        moved_plane = tile([P, S], U8, "moved_plane")
-        nc.vector.memset(moved_plane[:].bitcast(I32), 0)
+        scale_window = tile([P, T], U8, "scale_window", WINDOW - T // 2)
+        nc.vector.memset(scale_window[0 : 2 * QUAD, :].bitcast(I32), 0)
+        nc.vector.memset(scale_window[2 * QUAD : 3 * QUAD, :].bitcast(I32), 0)
+        tab_planes = tile([P, PASSES, S], U8, "tab_planes")
+        nc.vector.memset(tab_planes[:].rearrange("p a s -> p (a s)").bitcast(I32), 0)
 
         offsets = keep.tile([P, S // GROUP], U16, name="offsets")
-        word_window = [tile([P, T], U32, "word_window%d" % a, (0, "b")[a]) for a in range(PASSES)]
+        word_window = {}
         gate_window = {}
         dw_raw = {}
+        w4_codes = {}
 
         def picks(lo, hi):
             return offsets[:, lo // GROUP : hi // GROUP]
 
-        def load_words(a, lo=0, hi=T):
-            nc.sync.dma_start(word_window[a][:, lo:hi].bitcast(I32), tab_words[a].rearrange("p t i -> p (t i)").bitcast(I32)[:, lo:hi])
+        def load_words(a, slot):
+            word_window[a] = tile([P, T], U32, "word_window%d" % a, slot)
+            nc.sync.dma_start(word_window[a][:].bitcast(I32), tab_words[a].rearrange("p t i -> p (t i)").bitcast(I32))
 
         def load_gates(n, slot):
             gate_window[n] = tile([P, T], F32, "gate_window%d" % n, slot)
@@ -68,33 +73,26 @@ def tile_list_tabgate_none_kernel(tc, tab_words, tab_scales, w4_words, w4_scales
             dw_raw[a] = tile([P, PACK, M], F32, "dw_raw%d" % a, slot)
             nc.sync.dma_start(dw_raw[a][:], dw[a * K_PASS : (a + 1) * K_PASS, :].rearrange("(p i) n -> p i n", i=PACK))
 
-        w4_codes = {}
-
-        def load_w4(first, last):
+        def load_w4(first, last, slot):
             lo, hi = 2 * P * first, 2 * P * last
-            words = tile([P, PASSES, hi - lo], U8, "w4_codes%d" % first, "e" if first else 0)
+            words = tile([P, PASSES, hi - lo], U8, "w4_codes%d" % first, slot)
             nc.sync.dma_start(words[:].bitcast(I32), w4_words[:, :, lo:hi].rearrange("a p w -> p a w").bitcast(I32))
             for n in range(first, last):
                 for a in range(PASSES):
                     w4_codes[a, n] = words[:, a, 2 * P * (n - first) : 2 * P * (n - first + 1)]
 
         nc.sync.dma_start(offsets[:], offs)
-        load_words(0, 0, T // 2)
-        for q in range(4):
-            nc.sync.dma_start(scale_window[32 * q : 32 * q + 4, :].bitcast(I32), tab_scales[0, 4 * q : 4 * q + 4, :].bitcast(I32))
-        nc.sync.dma_start(scale_window[4:P:8, :].bitcast(I32), tab_scales[1].bitcast(I32))
-        load_words(0, T // 2, T)
-        load_dw(0, "d")
-        for q in range(4):
+        nc.sync.dma_start(scale_window[3 * QUAD : P, :].bitcast(I32), tab_scales.rearrange("a s t -> s a t").bitcast(I32))
+        load_words(0, "a")
+        for r in range(4):
             nc.sync.dma_start(
-                w4_planes[32 * q : 32 * q + 4, :, :].bitcast(I32),
-                w4_scales[:, 4 * q : 4 * q + 4, :].rearrange("a r n -> r a n").bitcast(I32),
+                w4_planes[r:P:QUAD, :, :].bitcast(I32),
+                w4_scales[:, r:16:4, :].rearrange("a q n -> q a n").bitcast(I32),
             )
-        load_dw(1, "c")
-        load_words(1)
+        load_words(1, "b")
+        load_w4(0, EARLY_TILES, None)
 
         gathered_scales = tile([P, S], U8, "gathered_scales")
-        tab_plane = [gathered_scales, moved_plane]
         tab_codes = [tile([P, S], U32, "tab_codes%d" % a) for a in range(PASSES)]
 
         def gather_words(a, lo, hi):
@@ -124,82 +122,64 @@ def tile_list_tabgate_none_kernel(tc, tab_words, tab_scales, w4_words, w4_scales
                 lhsT=codes,
                 lhsT_scale=plane,
                 rhs=tab_codes[a][:, lo:hi].bitcast(FP8X4),
-                rhs_scale=tab_plane[a][:, lo:hi],
+                rhs_scale=tab_planes[:, a, lo:hi],
                 start=start,
                 stop=stop,
             )
 
         acc = {}
 
-        def dw_pass(a, n, lo, hi, stop=False):
-            if a == 0:
-                acc[n, lo] = psum.tile([P, hi - lo], F32, name="acc%d_%d" % (n, lo), tag="bank%d" % (len(acc) % BANKS))
-            mx_pass(acc[n, lo][:], a, lo, hi, dw_codes[a, n][:].bitcast(FP8X4), dw_planes[a, n][:], a == 0, stop)
+        def open_sum(n, h):
+            acc[n, h] = psum.tile([P, HALF], F32, name="acc%d_%d" % (n, h), tag="bank%d_%d" % (n % 2, h))
 
-        def w4_pass(a, n, lo, hi, stop=False):
-            step = HALF if hi - lo == HALF else P
-            for j in range(lo, hi, step):
-                mx_pass(
-                    acc[n, lo][:, j - lo : j - lo + step], a, j, j + step,
-                    w4_codes[a, n].bitcast(FP4X4), w4_planes[:, a, n * P : (n + 1) * P], False, stop and j + step == hi,
-                )
+        def dw_pass(a, n, h, start, stop):
+            mx_pass(acc[n, h][:], a, h * HALF, (h + 1) * HALF, dw_codes[a, n][:].bitcast(FP8X4), dw_planes[a, n][:], start, stop)
+
+        def w4_pass(a, n, h, start, stop):
+            mx_pass(acc[n, h][:], a, h * HALF, (h + 1) * HALF, w4_codes[a, n].bitcast(FP4X4), w4_planes[:, a, n * P : (n + 1) * P], start, stop)
 
         def ranges(pieces):
             ends = list(accumulate(pieces))
             return list(zip([0] + ends, ends))
 
         nc.vector.tensor_copy(gathered_scales[:], scale_window[:].indirect(offsets[:]))
-        for q in range(4):
+        for q in (0, 2, 1, 3):
             nc.sync.dma_start(
-                moved_plane[32 * q : 32 * q + 4, :].bitcast(I32),
-                gathered_scales[32 * q + 4 : 32 * q + 32 : 8, :].bitcast(I32),
+                tab_planes[QUAD * q : QUAD * q + 4, :, :].bitcast(I32),
+                gathered_scales[3 * QUAD + 8 * q : 3 * QUAD + 8 * q + 8, :].bitcast(I32),
             )
-        for h in range(HALVES):
-            gather_words(0, h * HALF, (h + 1) * HALF)
-        load_w4(0, 2)
-        load_gates(0, PASSES * 2 * M)
+        load_dw(0, WINDOW)
+        load_dw(1, 0)
+        for a in range(PASSES):
+            for h in range(HALVES):
+                gather_words(a, h * HALF, (h + 1) * HALF)
+        load_gates(0, "a")
+        load_gates(1, "b")
         for n in range(ROW_TILES):
-            round_dw(0, n, nc.scalar.copy if n < ROW_TILES - 1 else nc.vector.tensor_copy, "e" if n % 2 else None)
+            round_dw(0, n, nc.vector.tensor_copy if n % 2 else nc.scalar.copy, "e" if n == 0 else None)
+        for n in range(ROW_TILES):
             quantize_dw(0, n)
-        load_gates(1, "d")
-        load_w4(2, ROW_TILES)
+        load_w4(EARLY_TILES, ROW_TILES, "e")
+        load_gates(2, WINDOW)
         for n in range(ROW_TILES):
             round_dw(1, n, nc.scalar.copy if n % 2 else nc.vector.tensor_copy)
-        for n in range(ROW_TILES):
             quantize_dw(1, n)
-        load_gates(2, "c")
-        for lo, hi in ranges(SUM_PIECES[0]):
-            gather_words(1, lo, hi)
-        load_gates(3, "b")
+        load_gates(3, 0)
 
-        sums = [(n, lo, hi) for n in range(ROW_TILES) for lo, hi in ranges(SUM_PIECES[n])]
-        for n, lo, hi in sums[:BANKS]:
-            dw_pass(0, n, lo, hi)
         ys = [tile([P, S], F32, "y%d" % n) for n in range(ROW_TILES)]
-
-        def close(n, lo, hi):
-            w4_pass(1, n, lo, hi)
-            dw_pass(1, n, lo, hi, True)
-
-        def copy_out(n, lo, hi):
-            nc.scalar.copy(ys[n][:, lo:hi], acc[n, lo][:])
-
-        for lo, hi in ranges(SUM_PIECES[0]):
-            w4_pass(0, 0, lo, hi)
-            close(0, lo, hi)
-            half = lo // HALF * HALF
-            if lo == half:
-                w4_pass(0, 1, half, half + HALF)
-            else:
-                close(1, half, half + HALF)
-            copy_out(0, lo, hi)
-        for n, lo, hi in sums[len(SUM_PIECES[0]) :]:
-            if (n, lo) not in acc:
-                dw_pass(0, n, lo, hi)
-            if n > 1:
-                w4_pass(0, n, lo, hi)
-                close(n, lo, hi)
-            copy_out(n, lo, hi)
+        orders = (
+            ((w4_pass, 0), (w4_pass, 1), (dw_pass, 0), (dw_pass, 1)),
+            ((w4_pass, 0), (w4_pass, 1), (dw_pass, 0), (dw_pass, 1)),
+            ((dw_pass, 0), (dw_pass, 1), (w4_pass, 0), (w4_pass, 1)),
+            ((w4_pass, 0), (w4_pass, 1), (dw_pass, 0), (dw_pass, 1)),
+        )
+        for n in range(ROW_TILES):
+            for h in range(HALVES):
+                open_sum(n, h)
+                for i, (one_pass, a) in enumerate(orders[n]):
+                    one_pass(a, n, h, i == 0, i == 2 * PASSES - 1)
+            for lo, hi in ranges(COPY_PIECES[n]):
+                nc.scalar.copy(ys[n][:, lo:hi], acc[n, lo // HALF][:, lo % HALF : lo % HALF + hi - lo])
         for n in range(ROW_TILES):
             result = tile([P, S], F32, "result%d" % n)
             for lo, hi in ranges(GATE_PIECES[n]):

@@ -44,13 +44,12 @@ def tile_list_tabgate_none_kernel(tc, tab_words, tab_scales, w4_words, w4_scales
                 return placed.tile(shape, dtype, name=name, offset=slot, align_bytes=256)
             return keep.tile(shape, dtype, name=name, tag=name if slot is None else "slot_" + slot, align_bytes=256)
 
-        w4_planes = tile([P, PASSES, M], U8, "w4_planes")
-        nc.vector.memset(w4_planes[:].rearrange("p a n -> p (a n)").bitcast(I32), 0)
-        scale_window = tile([P, T], U8, "scale_window", WINDOW - T // 2)
+        scale_window = tile([P, T], U8, "scale_window")
         nc.vector.memset(scale_window[0 : 2 * QUAD, :].bitcast(I32), 0)
         nc.vector.memset(scale_window[2 * QUAD : 3 * QUAD, :].bitcast(I32), 0)
-        tab_planes = tile([P, PASSES, S], U8, "tab_planes")
-        nc.vector.memset(tab_planes[:].rearrange("p a s -> p (a s)").bitcast(I32), 0)
+        planes = tile([P, PASSES, S + M], U8, "planes")
+        nc.vector.memset(planes[:].rearrange("p a s -> p (a s)").bitcast(I32), 0)
+        parked = tile([P, S + M], U8, "parked")
 
         offsets = keep.tile([P, S // GROUP], U16, name="offsets")
         word_window = {}
@@ -69,9 +68,10 @@ def tile_list_tabgate_none_kernel(tc, tab_words, tab_scales, w4_words, w4_scales
             gate_window[n] = tile([P, T], F32, "gate_window%d" % n, slot)
             nc.sync.dma_start(gate_window[n][:], gT[n * P : (n + 1) * P, :])
 
-        def load_dw(a, slot):
-            dw_raw[a] = tile([P, PACK, M], F32, "dw_raw%d" % a, slot)
-            nc.sync.dma_start(dw_raw[a][:], dw[a * K_PASS : (a + 1) * K_PASS, :].rearrange("(p i) n -> p i n", i=PACK))
+        def load_dw(a, slot, lo=0, hi=PACK):
+            if lo == 0:
+                dw_raw[a] = tile([P, PACK, M], F32, "dw_raw%d" % a, slot)
+            nc.sync.dma_start(dw_raw[a][:, lo:hi, :], dw[a * K_PASS : (a + 1) * K_PASS, :].rearrange("(p i) n -> p i n", i=PACK)[:, lo:hi, :])
 
         def load_w4(first, last, slot):
             lo, hi = 2 * P * first, 2 * P * last
@@ -84,15 +84,12 @@ def tile_list_tabgate_none_kernel(tc, tab_words, tab_scales, w4_words, w4_scales
         nc.sync.dma_start(offsets[:], offs)
         nc.sync.dma_start(scale_window[3 * QUAD : P, :].bitcast(I32), tab_scales.rearrange("a s t -> s a t").bitcast(I32))
         load_words(0, "a")
-        for r in range(4):
-            nc.sync.dma_start(
-                w4_planes[r:P:QUAD, :, :].bitcast(I32),
-                w4_scales[:, r:16:4, :].rearrange("a q n -> q a n").bitcast(I32),
-            )
+        nc.sync.dma_start(parked[3 * QUAD : P, S:].bitcast(I32), w4_scales.rearrange("a s n -> s a n").bitcast(I32))
         load_words(1, "b")
         load_w4(0, EARLY_TILES, None)
+        load_dw(0, "d", 0, PACK // 2)
 
-        gathered_scales = tile([P, S], U8, "gathered_scales")
+        gathered_scales = tile([P, S], U8, "gathered_scales", 0)
         tab_codes = [tile([P, S], U32, "tab_codes%d" % a) for a in range(PASSES)]
 
         def gather_words(a, lo, hi):
@@ -102,12 +99,13 @@ def tile_list_tabgate_none_kernel(tc, tab_words, tab_scales, w4_words, w4_scales
         dw_planes = {}
         dw_rounded = {}
 
-        def round_dw(a, n, copy, slot=None):
+        def round_dw(a, n, copy, slot=None, parts=1):
             dw_rounded[a, n] = tile([P, P, PACK], BF16, "dw_rounded%d_%d" % (a, n), slot)
-            copy(
-                dw_rounded[a, n][:].rearrange("p (c j) i -> p c i j", j=4),
-                dw_raw[a][:, :, n * P : (n + 1) * P].rearrange("p i (c j) -> p c i j", j=4),
-            )
+            for lo, hi in ranges([PACK // parts] * parts):
+                copy(
+                    dw_rounded[a, n][:, :, lo:hi].rearrange("p (c j) i -> p c i j", j=4),
+                    dw_raw[a][:, lo:hi, n * P : (n + 1) * P].rearrange("p i (c j) -> p c i j", j=4),
+                )
 
         def quantize_dw(a, n):
             dw_codes[a, n] = tile([P, P], U32, "dw_codes%d_%d" % (a, n))
@@ -122,7 +120,7 @@ def tile_list_tabgate_none_kernel(tc, tab_words, tab_scales, w4_words, w4_scales
                 lhsT=codes,
                 lhsT_scale=plane,
                 rhs=tab_codes[a][:, lo:hi].bitcast(FP8X4),
-                rhs_scale=tab_planes[:, a, lo:hi],
+                rhs_scale=planes[:, a, lo:hi],
                 start=start,
                 stop=stop,
             )
@@ -136,19 +134,20 @@ def tile_list_tabgate_none_kernel(tc, tab_words, tab_scales, w4_words, w4_scales
             mx_pass(acc[n, h][:], a, h * HALF, (h + 1) * HALF, dw_codes[a, n][:].bitcast(FP8X4), dw_planes[a, n][:], start, stop)
 
         def w4_pass(a, n, h, start, stop):
-            mx_pass(acc[n, h][:], a, h * HALF, (h + 1) * HALF, w4_codes[a, n].bitcast(FP4X4), w4_planes[:, a, n * P : (n + 1) * P], start, stop)
+            mx_pass(acc[n, h][:], a, h * HALF, (h + 1) * HALF, w4_codes[a, n].bitcast(FP4X4), planes[:, a, S + n * P : S + (n + 1) * P], start, stop)
 
         def ranges(pieces):
             ends = list(accumulate(pieces))
             return list(zip([0] + ends, ends))
 
         nc.vector.tensor_copy(gathered_scales[:], scale_window[:].indirect(offsets[:]))
+        nc.vector.tensor_copy(parked[3 * QUAD : P, :S].bitcast(I32), gathered_scales[3 * QUAD : P, :].bitcast(I32))
         for q in (0, 2, 1, 3):
             nc.sync.dma_start(
-                tab_planes[QUAD * q : QUAD * q + 4, :, :].bitcast(I32),
-                gathered_scales[3 * QUAD + 8 * q : 3 * QUAD + 8 * q + 8, :].bitcast(I32),
+                planes[QUAD * q : QUAD * q + 4, :, :].bitcast(I32),
+                parked[3 * QUAD + 8 * q : 3 * QUAD + 8 * q + 8, :].bitcast(I32),
             )
-        load_dw(0, WINDOW)
+        load_dw(0, "d", PACK // 2, PACK)
         load_dw(1, 0)
         for a in range(PASSES):
             for h in range(HALVES):
@@ -156,27 +155,25 @@ def tile_list_tabgate_none_kernel(tc, tab_words, tab_scales, w4_words, w4_scales
         load_gates(0, "a")
         load_gates(1, "b")
         for n in range(ROW_TILES):
-            round_dw(0, n, nc.vector.tensor_copy if n % 2 else nc.scalar.copy, "e" if n == 0 else None)
+            round_dw(0, n, nc.vector.tensor_copy if n % 2 else nc.scalar.copy, "e" if n == 0 else None, 2 if n == 0 else 1)
         for n in range(ROW_TILES):
             quantize_dw(0, n)
         load_w4(EARLY_TILES, ROW_TILES, "e")
-        load_gates(2, WINDOW)
+        load_gates(2, "d")
         for n in range(ROW_TILES):
             round_dw(1, n, nc.scalar.copy if n % 2 else nc.vector.tensor_copy)
             quantize_dw(1, n)
         load_gates(3, 0)
 
         ys = [tile([P, S], F32, "y%d" % n) for n in range(ROW_TILES)]
-        orders = (
-            ((w4_pass, 0), (w4_pass, 1), (dw_pass, 0), (dw_pass, 1)),
-            ((w4_pass, 0), (w4_pass, 1), (dw_pass, 0), (dw_pass, 1)),
-            ((dw_pass, 0), (dw_pass, 1), (w4_pass, 0), (w4_pass, 1)),
-            ((w4_pass, 0), (w4_pass, 1), (dw_pass, 0), (dw_pass, 1)),
-        )
+        w4_first = ((w4_pass, 0), (w4_pass, 1), (dw_pass, 0), (dw_pass, 1))
+        dw_first = ((dw_pass, 0), (dw_pass, 1), (w4_pass, 0), (w4_pass, 1))
+        late_first = ((dw_pass, 1), (dw_pass, 0), (w4_pass, 0), (w4_pass, 1))
+        orders = ((w4_first, w4_first), (w4_first, late_first), (dw_first, dw_first), (w4_first, w4_first))
         for n in range(ROW_TILES):
             for h in range(HALVES):
                 open_sum(n, h)
-                for i, (one_pass, a) in enumerate(orders[n]):
+                for i, (one_pass, a) in enumerate(orders[n][h]):
                     one_pass(a, n, h, i == 0, i == 2 * PASSES - 1)
             for lo, hi in ranges(COPY_PIECES[n]):
                 nc.scalar.copy(ys[n][:, lo:hi], acc[n, lo // HALF][:, lo % HALF : lo % HALF + hi - lo])

@@ -26,8 +26,9 @@ HALVES = S // HALF
 GROUP = 16
 QUAD = 32
 WINDOW = 4 * T
-GATE_PIECES = ([256, 256, 512], [1024], [1024], [512, 384, 128])
-COPY_PIECES = ([256, 256, 512], [512, 512], [512, 512], [512, 512])
+SUM_PIECES = ([256, 256, 512], [512, 512], [512, 512], [512, 512])
+GATE_PIECES = ([128, 384, 512], [1024], [1024], [512, 384, 128])
+COPY_PIECES = ([128, 128, 256, 512], [512, 512], [512, 512], [512, 512])
 EARLY_TILES = 2
 STORED_WHOLE = 3
 
@@ -127,14 +128,16 @@ def tile_list_tabgate_none_kernel(tc, tab_words, tab_scales, w4_words, w4_scales
 
         acc = {}
 
-        def open_sum(n, h):
-            acc[n, h] = psum.tile([P, HALF], F32, name="acc%d_%d" % (n, h), tag="bank%d_%d" % (n % 2, h))
+        def dw_pass(a, n, lo, hi, start, stop):
+            mx_pass(acc[n, lo][:], a, lo, hi, dw_codes[a, n][:].bitcast(FP8X4), dw_planes[a, n][:], start, stop)
 
-        def dw_pass(a, n, h, start, stop):
-            mx_pass(acc[n, h][:], a, h * HALF, (h + 1) * HALF, dw_codes[a, n][:].bitcast(FP8X4), dw_planes[a, n][:], start, stop)
-
-        def w4_pass(a, n, h, start, stop):
-            mx_pass(acc[n, h][:], a, h * HALF, (h + 1) * HALF, w4_codes[a, n].bitcast(FP4X4), planes[:, a, S + n * P : S + (n + 1) * P], start, stop)
+        def w4_pass(a, n, lo, hi, start, stop):
+            step = HALF if hi - lo == HALF else P
+            for j in range(lo, hi, step):
+                mx_pass(
+                    acc[n, lo][:, j - lo : j - lo + step], a, j, j + step, w4_codes[a, n].bitcast(FP4X4),
+                    planes[:, a, S + n * P : S + (n + 1) * P], start and j == lo, stop and j + step == hi,
+                )
 
         def ranges(pieces):
             ends = list(accumulate(pieces))
@@ -169,14 +172,16 @@ def tile_list_tabgate_none_kernel(tc, tab_words, tab_scales, w4_words, w4_scales
         w4_first = ((w4_pass, 0), (w4_pass, 1), (dw_pass, 0), (dw_pass, 1))
         dw_first = ((dw_pass, 0), (dw_pass, 1), (w4_pass, 0), (w4_pass, 1))
         late_first = ((dw_pass, 1), (dw_pass, 0), (w4_pass, 0), (w4_pass, 1))
-        orders = ((w4_first, w4_first), (w4_first, late_first), (dw_first, dw_first), (w4_first, w4_first))
+        orders = ((w4_first, w4_first, w4_first), (w4_first, late_first), (dw_first, dw_first), (w4_first, w4_first))
+        banks = ((0, 1, 2), (3, 4), (0, 2), (3, 4))
         for n in range(ROW_TILES):
-            for h in range(HALVES):
-                open_sum(n, h)
-                for i, (one_pass, a) in enumerate(orders[n][h]):
-                    one_pass(a, n, h, i == 0, i == 2 * PASSES - 1)
+            for (lo, hi), order, bank in zip(ranges(SUM_PIECES[n]), orders[n], banks[n]):
+                acc[n, lo] = psum.tile([P, hi - lo], F32, name="acc%d_%d" % (n, lo), tag="bank%d" % bank)
+                for i, (one_pass, a) in enumerate(order):
+                    one_pass(a, n, lo, hi, i == 0, i == 2 * PASSES - 1)
             for lo, hi in ranges(COPY_PIECES[n]):
-                nc.scalar.copy(ys[n][:, lo:hi], acc[n, lo // HALF][:, lo % HALF : lo % HALF + hi - lo])
+                first = max(start for tile_n, start in acc if tile_n == n and start <= lo)
+                nc.scalar.copy(ys[n][:, lo:hi], acc[n, first][:, lo - first : hi - first])
         for n in range(ROW_TILES):
             result = tile([P, S], F32, "result%d" % n)
             for lo, hi in ranges(GATE_PIECES[n]):

@@ -30,6 +30,7 @@ SUM_PIECES = ([256, 256, 512], [512, 512], [512, 512], [512, 512])
 GATE_PIECES = ([128, 384, 512], [1024], [1024], [512, 384, 128])
 COPY_PIECES = ([128, 128, 256, 512], [512, 512], [512, 512], [512, 512])
 EARLY_TILES = 2
+WARM_UPS = (0, HALF, HALF)
 STORED_WHOLE = 3
 
 
@@ -90,7 +91,7 @@ def tile_list_tabgate_none_kernel(tc, tab_words, tab_scales, w4_words, w4_scales
         load_w4(0, EARLY_TILES, None)
         load_dw(0, "d", 0, PACK // 2)
 
-        gathered_scales = tile([P, S], U8, "gathered_scales", 0)
+        gathered_scales = tile([P, S], U8, "gathered_scales")
         tab_codes = [tile([P, S], U32, "tab_codes%d" % a) for a in range(PASSES)]
 
         def gather_words(a, lo, hi):
@@ -155,11 +156,22 @@ def tile_list_tabgate_none_kernel(tc, tab_words, tab_scales, w4_words, w4_scales
         for a in range(PASSES):
             for h in range(HALVES):
                 gather_words(a, h * HALF, (h + 1) * HALF)
+        warm = psum.tile([P, HALF], F32, name="warm", tag="warm")
+        for i, lo in enumerate(WARM_UPS):
+            nc.tensor.matmul_mx(
+                out=warm[:],
+                lhsT=tab_codes[0][:, lo : lo + P].bitcast(FP8X4),
+                lhsT_scale=gathered_scales[:, lo : lo + P],
+                rhs=tab_codes[0][:, lo : lo + HALF].bitcast(FP8X4),
+                rhs_scale=gathered_scales[:, lo : lo + HALF],
+                start=i == 0,
+                stop=i == len(WARM_UPS) - 1,
+            )
         load_gates(0, "a")
         load_gates(1, "b")
         for n in range(ROW_TILES):
             round_dw(0, n, nc.vector.tensor_copy if n % 2 else nc.scalar.copy, "e" if n == 0 else None, 2 if n == 0 else 1)
-        for n in range(ROW_TILES):
+        for n in (0, 2, 3, 1):
             quantize_dw(0, n)
         load_w4(EARLY_TILES, ROW_TILES, "e")
         load_gates(2, "d")
@@ -171,7 +183,7 @@ def tile_list_tabgate_none_kernel(tc, tab_words, tab_scales, w4_words, w4_scales
         ys = [tile([P, S], F32, "y%d" % n) for n in range(ROW_TILES)]
         w4_first = ((w4_pass, 0), (w4_pass, 1), (dw_pass, 0), (dw_pass, 1))
         dw_first = ((dw_pass, 0), (dw_pass, 1), (w4_pass, 0), (w4_pass, 1))
-        late_first = ((dw_pass, 1), (dw_pass, 0), (w4_pass, 0), (w4_pass, 1))
+        late_first = ((w4_pass, 0), (dw_pass, 1), (dw_pass, 0), (w4_pass, 1))
         orders = ((w4_first, w4_first, w4_first), (w4_first, late_first), (dw_first, dw_first), (w4_first, w4_first))
         banks = ((0, 1, 2), (3, 4), (0, 2), (3, 4))
         for n in range(ROW_TILES):

@@ -27,11 +27,11 @@ GROUP = 16
 QUAD = 32
 WINDOW = 4 * T
 SUM_PIECES = ([256, 256, 512], [512, 512], [512, 512], [512, 512])
-GATE_PIECES = ([128, 384, 512], [1024], [1024], [512, 384, 128])
+GATE_PIECES = ([128, 384, 512], [1024], [1024], [512, 256, 128, 128])
 COPY_PIECES = ([128, 128, 256, 512], [512, 512], [512, 512], [512, 512])
 EARLY_TILES = 2
 WARM_UPS = (0, HALF, HALF)
-STORED_WHOLE = 3
+STORES = ((0, 2), (2, 3))
 
 
 def tile_list_tabgate_none_kernel(tc, tab_words, tab_scales, w4_words, w4_scales, dw, gT, offs, out):
@@ -194,11 +194,14 @@ def tile_list_tabgate_none_kernel(tc, tab_words, tab_scales, w4_words, w4_scales
             for lo, hi in ranges(COPY_PIECES[n]):
                 first = max(start for tile_n, start in acc if tile_n == n and start <= lo)
                 nc.scalar.copy(ys[n][:, lo:hi], acc[n, first][:, lo - first : hi - first])
-        for n in range(ROW_TILES):
-            result = tile([P, S], F32, "result%d" % n)
-            for lo, hi in ranges(GATE_PIECES[n]):
-                nc.vector.tensor_tensor(result[:, lo:hi], gate_window[n][:].indirect(picks(lo, hi)), ys[n][:, lo:hi], MULT)
-                if n >= STORED_WHOLE:
-                    nc.sync.dma_start(out[n * P : (n + 1) * P, lo:hi], result[:, lo:hi])
-            if n < STORED_WHOLE:
-                nc.sync.dma_start(out[n * P : (n + 1) * P, :], result[:])
+        for first, last in STORES:
+            result = tile([P, last - first, S], F32, "result%d" % first)
+            for n in range(first, last):
+                for lo, hi in ranges(GATE_PIECES[n]):
+                    nc.vector.tensor_tensor(result[:, n - first, lo:hi], gate_window[n][:].indirect(picks(lo, hi)), ys[n][:, lo:hi], MULT)
+            nc.sync.dma_start(out[first * P : last * P, :].rearrange("(n p) j -> p n j", p=P), result[:])
+        n = ROW_TILES - 1
+        result = tile([P, S], F32, "result%d" % n)
+        for lo, hi in ranges(GATE_PIECES[n]):
+            nc.vector.tensor_tensor(result[:, lo:hi], gate_window[n][:].indirect(picks(lo, hi)), ys[n][:, lo:hi], MULT)
+            nc.sync.dma_start(out[n * P : (n + 1) * P, lo:hi], result[:, lo:hi])

@@ -30,8 +30,8 @@ SUM_PIECES = ([256, 256, 512], [512, 512], [512, 512], [512, 512])
 GATE_PIECES = ([128, 384, 512], [1024], [1024], [512, 256, 128, 128])
 COPY_PIECES = ([128, 128, 256, 512], [512, 512], [512, 512], [512, 512])
 EARLY_TILES = 2
-WARM_UPS = (0, HALF, HALF)
-STORES = ((0, 2), (2, 3))
+EARLY_DW = 3
+WARM_UPS = (0, 0, HALF)
 
 
 def tile_list_tabgate_none_kernel(tc, tab_words, tab_scales, w4_words, w4_scales, dw, gT, offs, out):
@@ -70,10 +70,12 @@ def tile_list_tabgate_none_kernel(tc, tab_words, tab_scales, w4_words, w4_scales
             gate_window[n] = tile([P, T], F32, "gate_window%d" % n, slot)
             nc.sync.dma_start(gate_window[n][:], gT[n * P : (n + 1) * P, :])
 
-        def load_dw(a, slot, lo=0, hi=PACK):
-            if lo == 0:
-                dw_raw[a] = tile([P, PACK, M], F32, "dw_raw%d" % a, slot)
-            nc.sync.dma_start(dw_raw[a][:, lo:hi, :], dw[a * K_PASS : (a + 1) * K_PASS, :].rearrange("(p i) n -> p i n", i=PACK)[:, lo:hi, :])
+        def load_dw(a, first, last, slot):
+            raw = tile([P, PACK, P * (last - first)], F32, "dw_raw%d_%d" % (a, first), slot)
+            rows = dw[a * K_PASS : (a + 1) * K_PASS, :].rearrange("(p i) n -> p i n", i=PACK)
+            nc.sync.dma_start(raw[:], rows[:, :, P * first : P * last])
+            for n in range(first, last):
+                dw_raw[a, n] = raw[:, :, P * (n - first) : P * (n - first + 1)]
 
         def load_w4(first, last, slot):
             lo, hi = 2 * P * first, 2 * P * last
@@ -89,7 +91,7 @@ def tile_list_tabgate_none_kernel(tc, tab_words, tab_scales, w4_words, w4_scales
         nc.sync.dma_start(parked[3 * QUAD : P, S:].bitcast(I32), w4_scales.rearrange("a s n -> s a n").bitcast(I32))
         load_words(1, "b")
         load_w4(0, EARLY_TILES, None)
-        load_dw(0, "d", 0, PACK // 2)
+        load_dw(0, 0, EARLY_DW, None)
 
         gathered_scales = tile([P, S], U8, "gathered_scales")
         tab_codes = [tile([P, S], U32, "tab_codes%d" % a) for a in range(PASSES)]
@@ -101,13 +103,9 @@ def tile_list_tabgate_none_kernel(tc, tab_words, tab_scales, w4_words, w4_scales
         dw_planes = {}
         dw_rounded = {}
 
-        def round_dw(a, n, copy, slot=None, parts=1):
+        def round_dw(a, n, copy, slot=None):
             dw_rounded[a, n] = tile([P, P, PACK], BF16, "dw_rounded%d_%d" % (a, n), slot)
-            for lo, hi in ranges([PACK // parts] * parts):
-                copy(
-                    dw_rounded[a, n][:, :, lo:hi].rearrange("p (c j) i -> p c i j", j=4),
-                    dw_raw[a][:, lo:hi, n * P : (n + 1) * P].rearrange("p i (c j) -> p c i j", j=4),
-                )
+            copy(dw_rounded[a, n][:].rearrange("p (c j) i -> p c i j", j=4), dw_raw[a, n].rearrange("p i (c j) -> p c i j", j=4))
 
         def quantize_dw(a, n):
             dw_codes[a, n] = tile([P, P], U32, "dw_codes%d_%d" % (a, n))
@@ -151,8 +149,7 @@ def tile_list_tabgate_none_kernel(tc, tab_words, tab_scales, w4_words, w4_scales
                 planes[QUAD * q : QUAD * q + 4, :, :].bitcast(I32),
                 parked[3 * QUAD + 8 * q : 3 * QUAD + 8 * q + 8, :].bitcast(I32),
             )
-        load_dw(0, "d", PACK // 2, PACK)
-        load_dw(1, 0)
+        load_dw(1, 0, ROW_TILES, None)
         for a in range(PASSES):
             for h in range(HALVES):
                 gather_words(a, h * HALF, (h + 1) * HALF)
@@ -168,40 +165,73 @@ def tile_list_tabgate_none_kernel(tc, tab_words, tab_scales, w4_words, w4_scales
                 stop=i == len(WARM_UPS) - 1,
             )
         load_gates(0, "a")
-        load_gates(1, "b")
-        for n in range(ROW_TILES):
-            round_dw(0, n, nc.vector.tensor_copy if n % 2 else nc.scalar.copy, "e" if n == 0 else None, 2 if n == 0 else 1)
-        for n in (0, 2, 3, 1):
+        load_dw(0, EARLY_DW, ROW_TILES, "b")
+        for n in range(EARLY_DW):
+            round_dw(0, n, nc.scalar.copy)
             quantize_dw(0, n)
-        load_w4(EARLY_TILES, ROW_TILES, "e")
-        load_gates(2, "d")
+        load_gates(1, None)
         for n in range(ROW_TILES):
             round_dw(1, n, nc.scalar.copy if n % 2 else nc.vector.tensor_copy)
             quantize_dw(1, n)
-        load_gates(3, 0)
+        load_w4(EARLY_TILES, ROW_TILES, None)
+        load_gates(2, None)
+        load_gates(3, None)
 
         ys = [tile([P, S], F32, "y%d" % n) for n in range(ROW_TILES)]
-        w4_first = ((w4_pass, 0), (w4_pass, 1), (dw_pass, 0), (dw_pass, 1))
-        dw_first = ((dw_pass, 0), (dw_pass, 1), (w4_pass, 0), (w4_pass, 1))
-        late_first = ((w4_pass, 0), (dw_pass, 1), (dw_pass, 0), (w4_pass, 1))
-        orders = ((w4_first, w4_first, w4_first), (w4_first, late_first), (dw_first, dw_first), (w4_first, w4_first))
-        banks = ((0, 1, 2), (3, 4), (0, 2), (3, 4))
-        for n in range(ROW_TILES):
-            for (lo, hi), order, bank in zip(ranges(SUM_PIECES[n]), orders[n], banks[n]):
-                acc[n, lo] = psum.tile([P, hi - lo], F32, name="acc%d_%d" % (n, lo), tag="bank%d" % bank)
-                for i, (one_pass, a) in enumerate(order):
-                    one_pass(a, n, lo, hi, i == 0, i == 2 * PASSES - 1)
+        banks = ((0, 1, 2), (3, 4), (5, 6), (3, 4))
+        done = {}
+
+        def passes(one_pass, a, n, pieces=None):
+            for i, (lo, hi) in enumerate(ranges(SUM_PIECES[n])):
+                if pieces is None or i in pieces:
+                    count = done.get((n, lo), 0)
+                    if count == 0:
+                        acc[n, lo] = psum.tile([P, hi - lo], F32, name="acc%d_%d" % (n, lo), tag="bank%d" % banks[n][i])
+                    one_pass(a, n, lo, hi, count == 0, count == 2 * PASSES - 1)
+                    done[n, lo] = count + 1
+
+        def copy_sums(n):
             for lo, hi in ranges(COPY_PIECES[n]):
                 first = max(start for tile_n, start in acc if tile_n == n and start <= lo)
                 nc.scalar.copy(ys[n][:, lo:hi], acc[n, first][:, lo - first : hi - first])
-        for first, last in STORES:
-            result = tile([P, last - first, S], F32, "result%d" % first)
-            for n in range(first, last):
-                for lo, hi in ranges(GATE_PIECES[n]):
-                    nc.vector.tensor_tensor(result[:, n - first, lo:hi], gate_window[n][:].indirect(picks(lo, hi)), ys[n][:, lo:hi], MULT)
-            nc.sync.dma_start(out[first * P : last * P, :].rearrange("(n p) j -> p n j", p=P), result[:])
-        n = ROW_TILES - 1
-        result = tile([P, S], F32, "result%d" % n)
-        for lo, hi in ranges(GATE_PIECES[n]):
-            nc.vector.tensor_tensor(result[:, lo:hi], gate_window[n][:].indirect(picks(lo, hi)), ys[n][:, lo:hi], MULT)
-            nc.sync.dma_start(out[n * P : (n + 1) * P, lo:hi], result[:, lo:hi])
+
+        def late_sums(n, order, pieces=None):
+            for one_pass, a in order:
+                passes(one_pass, a, n, pieces)
+
+        dw_first = ((dw_pass, 1), (dw_pass, 0), (w4_pass, 0), (w4_pass, 1))
+        dw_around = ((dw_pass, 1), (w4_pass, 0), (w4_pass, 1), (dw_pass, 0))
+
+        def gate(n, result, store_pieces=False):
+            for lo, hi in ranges(GATE_PIECES[n]):
+                nc.vector.tensor_tensor(result[:, lo:hi], gate_window[n][:].indirect(picks(lo, hi)), ys[n][:, lo:hi], MULT)
+                if store_pieces:
+                    nc.sync.dma_start(out[n * P : (n + 1) * P, lo:hi], result[:, lo:hi])
+
+        first_two = tile([P, EARLY_TILES, S], F32, "result0")
+        passes(w4_pass, 0, 0)
+        passes(w4_pass, 0, 1, (0,))
+        passes(w4_pass, 1, 0, (0, 1))
+        passes(w4_pass, 1, 1, (0,))
+        passes(w4_pass, 1, 0, (2,))
+        passes(dw_pass, 0, 0)
+        passes(dw_pass, 1, 0)
+        copy_sums(0)
+        gate(0, first_two[:, 0, :])
+        round_dw(0, 3, nc.scalar.copy)
+        quantize_dw(0, 3)
+        passes(dw_pass, 0, 1, (0,))
+        passes(dw_pass, 1, 1, (0,))
+        late_sums(1, dw_first, (1,))
+        copy_sums(1)
+        gate(1, first_two[:, 1, :])
+        nc.sync.dma_start(out[: EARLY_TILES * P, :].rearrange("(n p) j -> p n j", p=P), first_two[:])
+        third = tile([P, S], F32, "result2")
+        for n, order in ((2, dw_first), (3, dw_around)):
+            for piece in range(HALVES):
+                late_sums(n, order, (piece,))
+            copy_sums(n)
+        gate(2, third[:])
+        nc.sync.dma_start(out[2 * P : 3 * P, :], third[:])
+        fourth = tile([P, S], F32, "result3")
+        gate(3, fourth[:], True)

@@ -31,7 +31,7 @@ GATE_PIECES = ([128, 384, 512], [1024], [1024], [512, 256, 128, 128])
 COPY_PIECES = ([128, 128, 256, 512], [512, 512], [512, 512], [512, 512])
 EARLY_TILES = 2
 EARLY_DW = 3
-WARM_UPS = (0, 0, HALF)
+WARM_UPS = ((0, HALF), (1, 0), (1, 0))
 
 
 def tile_list_tabgate_none_kernel(tc, tab_words, tab_scales, w4_words, w4_scales, dw, gT, offs, out):
@@ -154,12 +154,12 @@ def tile_list_tabgate_none_kernel(tc, tab_words, tab_scales, w4_words, w4_scales
             for h in range(HALVES):
                 gather_words(a, h * HALF, (h + 1) * HALF)
         warm = psum.tile([P, HALF], F32, name="warm", tag="warm")
-        for i, lo in enumerate(WARM_UPS):
+        for i, (a, lo) in enumerate(WARM_UPS):
             nc.tensor.matmul_mx(
                 out=warm[:],
-                lhsT=tab_codes[0][:, lo : lo + P].bitcast(FP8X4),
+                lhsT=tab_codes[a][:, lo : lo + P].bitcast(FP8X4),
                 lhsT_scale=gathered_scales[:, lo : lo + P],
-                rhs=tab_codes[0][:, lo : lo + HALF].bitcast(FP8X4),
+                rhs=tab_codes[a][:, lo : lo + HALF].bitcast(FP8X4),
                 rhs_scale=gathered_scales[:, lo : lo + HALF],
                 start=i == 0,
                 stop=i == len(WARM_UPS) - 1,
@@ -200,7 +200,8 @@ def tile_list_tabgate_none_kernel(tc, tab_words, tab_scales, w4_words, w4_scales
                 passes(one_pass, a, n, pieces)
 
         dw_first = ((dw_pass, 1), (dw_pass, 0), (w4_pass, 0), (w4_pass, 1))
-        dw_around = ((dw_pass, 1), (w4_pass, 0), (w4_pass, 1), (dw_pass, 0))
+        one_ahead = ((w4_pass, 0), (dw_pass, 1), (dw_pass, 0), (w4_pass, 1))
+        w4_first = ((w4_pass, 0), (w4_pass, 1), (dw_pass, 1), (dw_pass, 0))
 
         def gate(n, result, store_pieces=False):
             for lo, hi in ranges(GATE_PIECES[n]):
@@ -209,25 +210,19 @@ def tile_list_tabgate_none_kernel(tc, tab_words, tab_scales, w4_words, w4_scales
                     nc.sync.dma_start(out[n * P : (n + 1) * P, lo:hi], result[:, lo:hi])
 
         first_two = tile([P, EARLY_TILES, S], F32, "result0")
-        passes(w4_pass, 0, 0)
-        passes(w4_pass, 0, 1, (0,))
-        passes(w4_pass, 1, 0, (0, 1))
-        passes(w4_pass, 1, 1, (0,))
-        passes(w4_pass, 1, 0, (2,))
-        passes(dw_pass, 0, 0)
-        passes(dw_pass, 1, 0)
+        for one_pass, a in ((w4_pass, 0), (w4_pass, 1), (dw_pass, 0), (dw_pass, 1)):
+            passes(one_pass, a, 0)
         copy_sums(0)
         gate(0, first_two[:, 0, :])
         round_dw(0, 3, nc.scalar.copy)
         quantize_dw(0, 3)
-        passes(dw_pass, 0, 1, (0,))
-        passes(dw_pass, 1, 1, (0,))
+        late_sums(1, one_ahead, (0,))
         late_sums(1, dw_first, (1,))
         copy_sums(1)
         gate(1, first_two[:, 1, :])
         nc.sync.dma_start(out[: EARLY_TILES * P, :].rearrange("(n p) j -> p n j", p=P), first_two[:])
         third = tile([P, S], F32, "result2")
-        for n, order in ((2, dw_first), (3, dw_around)):
+        for n, order in ((2, dw_first), (3, w4_first)):
             for piece in range(HALVES):
                 late_sums(n, order, (piece,))
             copy_sums(n)

@@ -27,11 +27,11 @@ GROUP = 16
 QUAD = 32
 WINDOW = 4 * T
 SUM_PIECES = ([256, 256, 512], [512, 512], [512, 512], [512, 512])
-GATE_PIECES = ([128, 384, 512], [1024], [1024], [512, 256, 128, 128])
-COPY_PIECES = ([128, 128, 256, 512], [512, 512], [512, 512], [512, 512])
+GATE_PIECES = ([384, 640], [1024], [1024], [512, 256, 128, 128])
+COPY_PIECES = ([256, 128, 128, 512], [512, 512], [512, 512], [512, 512])
 EARLY_TILES = 2
-EARLY_DW = 3
-WARM_UPS = ((0, HALF), (1, 0), (1, 0))
+EARLY_DW = 2
+WARM_UPS = ((0, HALF), (0, HALF), (1, 0))
 
 
 def tile_list_tabgate_none_kernel(tc, tab_words, tab_scales, w4_words, w4_scales, dw, gT, offs, out):
@@ -70,10 +70,11 @@ def tile_list_tabgate_none_kernel(tc, tab_words, tab_scales, w4_words, w4_scales
             gate_window[n] = tile([P, T], F32, "gate_window%d" % n, slot)
             nc.sync.dma_start(gate_window[n][:], gT[n * P : (n + 1) * P, :])
 
-        def load_dw(a, first, last, slot):
-            raw = tile([P, PACK, P * (last - first)], F32, "dw_raw%d_%d" % (a, first), slot)
+        def load_dw(a, first, last, raw=None):
+            if raw is None:
+                raw = tile([P, PACK, P * (last - first)], F32, "dw_raw%d_%d" % (a, first))[:]
             rows = dw[a * K_PASS : (a + 1) * K_PASS, :].rearrange("(p i) n -> p i n", i=PACK)
-            nc.sync.dma_start(raw[:], rows[:, :, P * first : P * last])
+            nc.sync.dma_start(raw, rows[:, :, P * first : P * last])
             for n in range(first, last):
                 dw_raw[a, n] = raw[:, :, P * (n - first) : P * (n - first + 1)]
 
@@ -91,7 +92,7 @@ def tile_list_tabgate_none_kernel(tc, tab_words, tab_scales, w4_words, w4_scales
         nc.sync.dma_start(parked[3 * QUAD : P, S:].bitcast(I32), w4_scales.rearrange("a s n -> s a n").bitcast(I32))
         load_words(1, "b")
         load_w4(0, EARLY_TILES, None)
-        load_dw(0, 0, EARLY_DW, None)
+        load_dw(0, 0, EARLY_DW)
 
         gathered_scales = tile([P, S], U8, "gathered_scales")
         tab_codes = [tile([P, S], U32, "tab_codes%d" % a) for a in range(PASSES)]
@@ -131,12 +132,7 @@ def tile_list_tabgate_none_kernel(tc, tab_words, tab_scales, w4_words, w4_scales
             mx_pass(acc[n, lo][:], a, lo, hi, dw_codes[a, n][:].bitcast(FP8X4), dw_planes[a, n][:], start, stop)
 
         def w4_pass(a, n, lo, hi, start, stop):
-            step = HALF if hi - lo == HALF else P
-            for j in range(lo, hi, step):
-                mx_pass(
-                    acc[n, lo][:, j - lo : j - lo + step], a, j, j + step, w4_codes[a, n].bitcast(FP4X4),
-                    planes[:, a, S + n * P : S + (n + 1) * P], start and j == lo, stop and j + step == hi,
-                )
+            mx_pass(acc[n, lo][:], a, lo, hi, w4_codes[a, n].bitcast(FP4X4), planes[:, a, S + n * P : S + (n + 1) * P], start, stop)
 
         def ranges(pieces):
             ends = list(accumulate(pieces))
@@ -149,7 +145,7 @@ def tile_list_tabgate_none_kernel(tc, tab_words, tab_scales, w4_words, w4_scales
                 planes[QUAD * q : QUAD * q + 4, :, :].bitcast(I32),
                 parked[3 * QUAD + 8 * q : 3 * QUAD + 8 * q + 8, :].bitcast(I32),
             )
-        load_dw(1, 0, ROW_TILES, None)
+        load_dw(1, 0, ROW_TILES)
         for a in range(PASSES):
             for h in range(HALVES):
                 gather_words(a, h * HALF, (h + 1) * HALF)
@@ -165,7 +161,8 @@ def tile_list_tabgate_none_kernel(tc, tab_words, tab_scales, w4_words, w4_scales
                 stop=i == len(WARM_UPS) - 1,
             )
         load_gates(0, "a")
-        load_dw(0, EARLY_DW, ROW_TILES, "b")
+        shared = tile([P, HALF + S], F32, "shared", "b")
+        load_dw(0, EARLY_DW, ROW_TILES, shared[:, HALF:].rearrange("p (i n) -> p i n", i=PACK))
         for n in range(EARLY_DW):
             round_dw(0, n, nc.scalar.copy)
             quantize_dw(0, n)
@@ -177,7 +174,7 @@ def tile_list_tabgate_none_kernel(tc, tab_words, tab_scales, w4_words, w4_scales
         load_gates(2, None)
         load_gates(3, None)
 
-        ys = [tile([P, S], F32, "y%d" % n) for n in range(ROW_TILES)]
+        ys = [shared[:, :S] if n == 1 else tile([P, S], F32, "y%d" % n)[:] for n in range(ROW_TILES)]
         banks = ((0, 1, 2), (3, 4), (5, 6), (3, 4))
         done = {}
 
@@ -201,7 +198,7 @@ def tile_list_tabgate_none_kernel(tc, tab_words, tab_scales, w4_words, w4_scales
 
         dw_first = ((dw_pass, 1), (dw_pass, 0), (w4_pass, 0), (w4_pass, 1))
         one_ahead = ((w4_pass, 0), (dw_pass, 1), (dw_pass, 0), (w4_pass, 1))
-        w4_first = ((w4_pass, 0), (w4_pass, 1), (dw_pass, 1), (dw_pass, 0))
+        dw_around = ((dw_pass, 1), (w4_pass, 0), (w4_pass, 1), (dw_pass, 0))
 
         def gate(n, result, store_pieces=False):
             for lo, hi in ranges(GATE_PIECES[n]):
@@ -214,15 +211,16 @@ def tile_list_tabgate_none_kernel(tc, tab_words, tab_scales, w4_words, w4_scales
             passes(one_pass, a, 0)
         copy_sums(0)
         gate(0, first_two[:, 0, :])
-        round_dw(0, 3, nc.scalar.copy)
-        quantize_dw(0, 3)
         late_sums(1, one_ahead, (0,))
         late_sums(1, dw_first, (1,))
+        for n in range(EARLY_DW, ROW_TILES):
+            round_dw(0, n, nc.scalar.copy)
+            quantize_dw(0, n)
         copy_sums(1)
         gate(1, first_two[:, 1, :])
         nc.sync.dma_start(out[: EARLY_TILES * P, :].rearrange("(n p) j -> p n j", p=P), first_two[:])
         third = tile([P, S], F32, "result2")
-        for n, order in ((2, dw_first), (3, w4_first)):
+        for n, order in ((2, dw_first), (3, dw_around)):
             for piece in range(HALVES):
                 late_sums(n, order, (piece,))
             copy_sums(n)

@@ -26,9 +26,9 @@ HALVES = S // HALF
 GROUP = 16
 QUAD = 32
 WINDOW = 4 * T
-SUM_PIECES = ([256, 256, 512], [512, 512], [512, 512], [512, 512])
-GATE_PIECES = ([384, 640], [1024], [1024], [512, 256, 128, 128])
-COPY_PIECES = ([256, 128, 128, 512], [512, 512], [512, 512], [512, 512])
+SUM_PIECES = ([256, 256, 512], [512, 512], [256, 256, 256, 256], [512, 512])
+GATE_PIECES = ([384, 640], [512, 512], [1024], [512, 256, 128, 128])
+COPY_PIECES = ([256, 128, 128, 512], [512, 512], [256, 256, 256, 256], [512, 512])
 EARLY_TILES = 2
 EARLY_DW = 2
 WARM_UPS = ((0, HALF), (0, HALF), (1, 0))
@@ -175,7 +175,7 @@ def tile_list_tabgate_none_kernel(tc, tab_words, tab_scales, w4_words, w4_scales
         load_gates(3, None)
 
         ys = [shared[:, :S] if n == 1 else tile([P, S], F32, "y%d" % n)[:] for n in range(ROW_TILES)]
-        banks = ((0, 1, 2), (3, 4), (5, 6), (3, 4))
+        banks = ((0, 1, 2), (3, 4), (5, 6, 0, 1), (3, 4))
         done = {}
 
         def passes(one_pass, a, n, pieces=None):
@@ -198,7 +198,7 @@ def tile_list_tabgate_none_kernel(tc, tab_words, tab_scales, w4_words, w4_scales
 
         dw_first = ((dw_pass, 1), (dw_pass, 0), (w4_pass, 0), (w4_pass, 1))
         one_ahead = ((w4_pass, 0), (dw_pass, 1), (dw_pass, 0), (w4_pass, 1))
-        dw_around = ((dw_pass, 1), (w4_pass, 0), (w4_pass, 1), (dw_pass, 0))
+        w4_first = ((w4_pass, 0), (w4_pass, 1), (dw_pass, 1), (dw_pass, 0))
 
         def gate(n, result, store_pieces=False):
             for lo, hi in ranges(GATE_PIECES[n]):
@@ -220,8 +220,8 @@ def tile_list_tabgate_none_kernel(tc, tab_words, tab_scales, w4_words, w4_scales
         gate(1, first_two[:, 1, :])
         nc.sync.dma_start(out[: EARLY_TILES * P, :].rearrange("(n p) j -> p n j", p=P), first_two[:])
         third = tile([P, S], F32, "result2")
-        for n, order in ((2, dw_first), (3, dw_around)):
-            for piece in range(HALVES):
+        for n, order in ((2, dw_first), (3, w4_first)):
+            for piece in range(len(SUM_PIECES[n])):
                 late_sums(n, order, (piece,))
             copy_sums(n)
         gate(2, third[:])

@@ -26,10 +26,10 @@ HALVES = S // HALF
 GROUP = 16
 QUAD = 32
 WINDOW = 4 * T
-SUM_PIECES = ([256, 256, 512], [512, 512], [256, 256, 256, 256], [512, 512])
-GATE_PIECES = ([384, 640], [512, 512], [1024], [512, 256, 128, 128])
-COPY_PIECES = ([256, 128, 128, 512], [512, 512], [256, 256, 256, 256], [512, 512])
-EARLY_TILES = 2
+SUM_PIECES = ([256, 256, 512], [512, 512], [512, 512], [512, 512])
+GATE_PIECES = ([384, 640], [512, 512], [1024], [512, 320, 192])
+COPY_PIECES = ([256, 128, 128, 512], [512, 512], [512, 512], [512, 512])
+EARLY_TILES = 3
 EARLY_DW = 2
 WARM_UPS = ((0, HALF), (0, HALF), (1, 0))
 
@@ -145,7 +145,7 @@ def tile_list_tabgate_none_kernel(tc, tab_words, tab_scales, w4_words, w4_scales
                 planes[QUAD * q : QUAD * q + 4, :, :].bitcast(I32),
                 parked[3 * QUAD + 8 * q : 3 * QUAD + 8 * q + 8, :].bitcast(I32),
             )
-        load_dw(1, 0, ROW_TILES)
+        load_dw(1, 0, ROW_TILES - 1)
         for a in range(PASSES):
             for h in range(HALVES):
                 gather_words(a, h * HALF, (h + 1) * HALF)
@@ -167,15 +167,16 @@ def tile_list_tabgate_none_kernel(tc, tab_words, tab_scales, w4_words, w4_scales
             round_dw(0, n, nc.scalar.copy)
             quantize_dw(0, n)
         load_gates(1, None)
-        for n in range(ROW_TILES):
+        for n in range(ROW_TILES - 1):
             round_dw(1, n, nc.scalar.copy if n % 2 else nc.vector.tensor_copy)
             quantize_dw(1, n)
-        load_w4(EARLY_TILES, ROW_TILES, None)
+        load_dw(1, ROW_TILES - 1, ROW_TILES, tile([P, PACK, P], F32, "dw_last", "late")[:])
         load_gates(2, None)
+        load_w4(EARLY_TILES, ROW_TILES, None)
         load_gates(3, None)
 
-        ys = [shared[:, :S] if n == 1 else tile([P, S], F32, "y%d" % n)[:] for n in range(ROW_TILES)]
-        banks = ((0, 1, 2), (3, 4), (5, 6, 0, 1), (3, 4))
+        ys = {1: shared[:, :S]}
+        banks = ((0, 1, 2), (3, 4), (5, 6), (5, 6))
         done = {}
 
         def passes(one_pass, a, n, pieces=None):
@@ -188,6 +189,8 @@ def tile_list_tabgate_none_kernel(tc, tab_words, tab_scales, w4_words, w4_scales
                     done[n, lo] = count + 1
 
         def copy_sums(n):
+            if n not in ys:
+                ys[n] = tile([P, S], F32, "y%d" % n, "late" if n == 2 else None)[:]
             for lo, hi in ranges(COPY_PIECES[n]):
                 first = max(start for tile_n, start in acc if tile_n == n and start <= lo)
                 nc.scalar.copy(ys[n][:, lo:hi], acc[n, first][:, lo - first : hi - first])
@@ -197,8 +200,8 @@ def tile_list_tabgate_none_kernel(tc, tab_words, tab_scales, w4_words, w4_scales
                 passes(one_pass, a, n, pieces)
 
         dw_first = ((dw_pass, 1), (dw_pass, 0), (w4_pass, 0), (w4_pass, 1))
-        one_ahead = ((w4_pass, 0), (dw_pass, 1), (dw_pass, 0), (w4_pass, 1))
-        w4_first = ((w4_pass, 0), (w4_pass, 1), (dw_pass, 1), (dw_pass, 0))
+        pass_0_last = ((dw_pass, 1), (w4_pass, 0), (w4_pass, 1), (dw_pass, 0))
+        pass_1_last = ((dw_pass, 0), (w4_pass, 0), (w4_pass, 1), (dw_pass, 1))
 
         def gate(n, result, store_pieces=False):
             for lo, hi in ranges(GATE_PIECES[n]):
@@ -206,21 +209,23 @@ def tile_list_tabgate_none_kernel(tc, tab_words, tab_scales, w4_words, w4_scales
                 if store_pieces:
                     nc.sync.dma_start(out[n * P : (n + 1) * P, lo:hi], result[:, lo:hi])
 
-        first_two = tile([P, EARLY_TILES, S], F32, "result0")
+        first_two = tile([P, 2, S], F32, "result0")
         for one_pass, a in ((w4_pass, 0), (w4_pass, 1), (dw_pass, 0), (dw_pass, 1)):
             passes(one_pass, a, 0)
         copy_sums(0)
         gate(0, first_two[:, 0, :])
-        late_sums(1, one_ahead, (0,))
+        late_sums(1, dw_first, (0,))
         late_sums(1, dw_first, (1,))
         for n in range(EARLY_DW, ROW_TILES):
             round_dw(0, n, nc.scalar.copy)
             quantize_dw(0, n)
         copy_sums(1)
         gate(1, first_two[:, 1, :])
-        nc.sync.dma_start(out[: EARLY_TILES * P, :].rearrange("(n p) j -> p n j", p=P), first_two[:])
+        round_dw(1, 3, nc.scalar.copy)
+        quantize_dw(1, 3)
+        nc.sync.dma_start(out[: 2 * P, :].rearrange("(n p) j -> p n j", p=P), first_two[:])
         third = tile([P, S], F32, "result2")
-        for n, order in ((2, dw_first), (3, w4_first)):
+        for n, order in ((2, pass_0_last), (3, pass_1_last)):
             for piece in range(len(SUM_PIECES[n])):
                 late_sums(n, order, (piece,))
             copy_sums(n)

@@ -26,9 +26,9 @@ HALVES = S // HALF
 GROUP = 16
 QUAD = 32
 WINDOW = 4 * T
-SUM_PIECES = ([256, 256, 512], [512, 512], [512, 512], [512, 512])
+SUM_PIECES = ([256, 256, 512], [512, 512], [256, 256, 512], [256, 256, 512])
 GATE_PIECES = ([384, 640], [512, 512], [1024], [512, 320, 192])
-COPY_PIECES = ([256, 128, 128, 512], [512, 512], [512, 512], [512, 512])
+COPY_PIECES = ([256, 128, 128, 512], [512, 512], [256, 256, 512], [256, 256, 512])
 EARLY_TILES = 3
 EARLY_DW = 2
 WARM_UPS = ((0, HALF), (0, HALF), (1, 0))
@@ -176,7 +176,7 @@ def tile_list_tabgate_none_kernel(tc, tab_words, tab_scales, w4_words, w4_scales
         load_gates(3, None)
 
         ys = {1: shared[:, :S]}
-        banks = ((0, 1, 2), (3, 4), (5, 6), (5, 6))
+        banks = ((0, 1, 2), (3, 4), (5, 0, 6), (5, 0, 6))
         done = {}
 
         def passes(one_pass, a, n, pieces=None):

from contextlib import ExitStack
from itertools import accumulate

import concourse.mybir as mybir

K, M, T, S = 1024, 512, 2048, 1024
FLOPS = 2 * 2 * K * M * S

F32 = mybir.dt.float32
BF16 = mybir.dt.bfloat16
I32 = mybir.dt.int32
U32 = mybir.dt.uint32
U16 = mybir.dt.uint16
U8 = mybir.dt.uint8
FP8X4 = mybir.dt.float8_e4m3fn_x4
FP4X4 = mybir.dt.float4_e2m1fn_x4
MULT = mybir.AluOpType.mult

P = 128
PACK = 4
K_PASS = P * PACK
PASSES = K // K_PASS
ROW_TILES = M // P
HALF = 512
HALVES = S // HALF
GROUP = 16
QUAD = 32
WINDOW = 4 * T
SUM_PIECES = ([256, 256, 512], [512, 512], [256, 256, 512], [256, 256, 512])
GATE_PIECES = ([384, 640], [512, 512], [1024], [512, 320, 192])
COPY_PIECES = ([256, 128, 128, 512], [512, 512], [256, 256, 512], [256, 256, 512])
EARLY_TILES = 3
EARLY_DW = 2
WARM_UPS = ((0, HALF), (0, HALF), (1, 0))


def tile_list_tabgate_none_kernel(tc, tab_words, tab_scales, w4_words, w4_scales, dw, gT, offs, out):
    nc = tc.nc
    with ExitStack() as ctx:
        keep = ctx.enter_context(tc.tile_pool(name="keep", bufs=1))
        placed = ctx.enter_context(tc.tile_pool(name="placed", bufs=1))
        psum = ctx.enter_context(tc.psum_pool(name="psum", bufs=1))

        def tile(shape, dtype, name, slot=None):
            if isinstance(slot, int):
                return placed.tile(shape, dtype, name=name, offset=slot, align_bytes=256)
            return keep.tile(shape, dtype, name=name, tag=name if slot is None else "slot_" + slot, align_bytes=256)

        scale_window = tile([P, T], U8, "scale_window")
        nc.vector.memset(scale_window[0 : 2 * QUAD, :].bitcast(I32), 0)
        nc.vector.memset(scale_window[2 * QUAD : 3 * QUAD, :].bitcast(I32), 0)
        planes = tile([P, PASSES, S + M], U8, "planes")
        nc.vector.memset(planes[:].rearrange("p a s -> p (a s)").bitcast(I32), 0)
        parked = tile([P, S + M], U8, "parked")

        offsets = keep.tile([P, S // GROUP], U16, name="offsets")
        word_window = {}
        gate_window = {}
        dw_raw = {}
        w4_codes = {}

        def picks(lo, hi):
            return offsets[:, lo // GROUP : hi // GROUP]

        def load_words(a, slot):
            word_window[a] = tile([P, T], U32, "word_window%d" % a, slot)
            nc.sync.dma_start(word_window[a][:].bitcast(I32), tab_words[a].rearrange("p t i -> p (t i)").bitcast(I32))

        def load_gates(n, slot):
            gate_window[n] = tile([P, T], F32, "gate_window%d" % n, slot)
            nc.sync.dma_start(gate_window[n][:], gT[n * P : (n + 1) * P, :])

        def load_dw(a, first, last, raw=None):
            if raw is None:
                raw = tile([P, PACK, P * (last - first)], F32, "dw_raw%d_%d" % (a, first))[:]
            rows = dw[a * K_PASS : (a + 1) * K_PASS, :].rearrange("(p i) n -> p i n", i=PACK)
            nc.sync.dma_start(raw, rows[:, :, P * first : P * last])
            for n in range(first, last):
                dw_raw[a, n] = raw[:, :, P * (n - first) : P * (n - first + 1)]

        def load_w4(first, last, slot):
            lo, hi = 2 * P * first, 2 * P * last
            words = tile([P, PASSES, hi - lo], U8, "w4_codes%d" % first, slot)
            nc.sync.dma_start(words[:].bitcast(I32), w4_words[:, :, lo:hi].rearrange("a p w -> p a w").bitcast(I32))
            for n in range(first, last):
                for a in range(PASSES):
                    w4_codes[a, n] = words[:, a, 2 * P * (n - first) : 2 * P * (n - first + 1)]

        nc.sync.dma_start(offsets[:], offs)
        nc.sync.dma_start(scale_window[3 * QUAD : P, :].bitcast(I32), tab_scales.rearrange("a s t -> s a t").bitcast(I32))
        load_words(0, "a")
        nc.sync.dma_start(parked[3 * QUAD : P, S:].bitcast(I32), w4_scales.rearrange("a s n -> s a n").bitcast(I32))
        load_words(1, "b")
        load_w4(0, EARLY_TILES, None)
        load_dw(0, 0, EARLY_DW)

        gathered_scales = tile([P, S], U8, "gathered_scales")
        tab_codes = [tile([P, S], U32, "tab_codes%d" % a) for a in range(PASSES)]

        def gather_words(a, lo, hi):
            nc.vector.tensor_copy(tab_codes[a][:, lo:hi], word_window[a][:].indirect(picks(lo, hi)))

        dw_codes = {}
        dw_planes = {}
        dw_rounded = {}

        def round_dw(a, n, copy, slot=None):
            dw_rounded[a, n] = tile([P, P, PACK], BF16, "dw_rounded%d_%d" % (a, n), slot)
            copy(dw_rounded[a, n][:].rearrange("p (c j) i -> p c i j", j=4), dw_raw[a, n].rearrange("p i (c j) -> p c i j", j=4))

        def quantize_dw(a, n):
            dw_codes[a, n] = tile([P, P], U32, "dw_codes%d_%d" % (a, n))
            dw_planes[a, n] = tile([P, P], U8, "dw_plane%d_%d" % (a, n))
            nc.vector.quantize_mx(
                out=dw_codes[a, n][:].bitcast(FP8X4), scales=dw_planes[a, n][:], in_=dw_rounded[a, n][:].rearrange("p c i -> p (c i)")
            )

        def mx_pass(acc, a, lo, hi, codes, plane, start, stop):
            nc.tensor.matmul_mx(
                out=acc,
                lhsT=codes,
                lhsT_scale=plane,
                rhs=tab_codes[a][:, lo:hi].bitcast(FP8X4),
                rhs_scale=planes[:, a, lo:hi],
                start=start,
                stop=stop,
            )

        acc = {}

        def dw_pass(a, n, lo, hi, start, stop):
            mx_pass(acc[n, lo][:], a, lo, hi, dw_codes[a, n][:].bitcast(FP8X4), dw_planes[a, n][:], start, stop)

        def w4_pass(a, n, lo, hi, start, stop):
            mx_pass(acc[n, lo][:], a, lo, hi, w4_codes[a, n].bitcast(FP4X4), planes[:, a, S + n * P : S + (n + 1) * P], start, stop)

        def ranges(pieces):
            ends = list(accumulate(pieces))
            return list(zip([0] + ends, ends))

        nc.vector.tensor_copy(gathered_scales[:], scale_window[:].indirect(offsets[:]))
        nc.vector.tensor_copy(parked[3 * QUAD : P, :S].bitcast(I32), gathered_scales[3 * QUAD : P, :].bitcast(I32))
        for q in (0, 2, 1, 3):
            nc.sync.dma_start(
                planes[QUAD * q : QUAD * q + 4, :, :].bitcast(I32),
                parked[3 * QUAD + 8 * q : 3 * QUAD + 8 * q + 8, :].bitcast(I32),
            )
        load_dw(1, 0, ROW_TILES - 1)
        for a in range(PASSES):
            for h in range(HALVES):
                gather_words(a, h * HALF, (h + 1) * HALF)
        warm = psum.tile([P, HALF], F32, name="warm", tag="warm")
        for i, (a, lo) in enumerate(WARM_UPS):
            nc.tensor.matmul_mx(
                out=warm[:],
                lhsT=tab_codes[a][:, lo : lo + P].bitcast(FP8X4),
                lhsT_scale=gathered_scales[:, lo : lo + P],
                rhs=tab_codes[a][:, lo : lo + HALF].bitcast(FP8X4),
                rhs_scale=gathered_scales[:, lo : lo + HALF],
                start=i == 0,
                stop=i == len(WARM_UPS) - 1,
            )
        load_gates(0, "a")
        shared = tile([P, HALF + S], F32, "shared", "b")
        load_dw(0, EARLY_DW, ROW_TILES, shared[:, HALF:].rearrange("p (i n) -> p i n", i=PACK))
        for n in range(EARLY_DW):
            round_dw(0, n, nc.scalar.copy)
            quantize_dw(0, n)
        load_gates(1, None)
        for n in range(ROW_TILES - 1):
            round_dw(1, n, nc.scalar.copy if n % 2 else nc.vector.tensor_copy)
            quantize_dw(1, n)
        load_dw(1, ROW_TILES - 1, ROW_TILES, tile([P, PACK, P], F32, "dw_last", "late")[:])
        load_gates(2, None)
        load_w4(EARLY_TILES, ROW_TILES, None)
        load_gates(3, None)

        ys = {1: shared[:, :S]}
        banks = ((0, 1, 2), (3, 4), (5, 0, 6), (5, 0, 6))
        done = {}

        def passes(one_pass, a, n, pieces=None):
            for i, (lo, hi) in enumerate(ranges(SUM_PIECES[n])):
                if pieces is None or i in pieces:
                    count = done.get((n, lo), 0)
                    if count == 0:
                        acc[n, lo] = psum.tile([P, hi - lo], F32, name="acc%d_%d" % (n, lo), tag="bank%d" % banks[n][i])
                    one_pass(a, n, lo, hi, count == 0, count == 2 * PASSES - 1)
                    done[n, lo] = count + 1

        def copy_sums(n):
            if n not in ys:
                ys[n] = tile([P, S], F32, "y%d" % n, "late" if n == 2 else None)[:]
            for lo, hi in ranges(COPY_PIECES[n]):
                first = max(start for tile_n, start in acc if tile_n == n and start <= lo)
                nc.scalar.copy(ys[n][:, lo:hi], acc[n, first][:, lo - first : hi - first])

        def late_sums(n, order, pieces=None):
            for one_pass, a in order:
                passes(one_pass, a, n, pieces)

        dw_first = ((dw_pass, 1), (dw_pass, 0), (w4_pass, 0), (w4_pass, 1))
        pass_0_last = ((dw_pass, 1), (w4_pass, 0), (w4_pass, 1), (dw_pass, 0))
        pass_1_last = ((dw_pass, 0), (w4_pass, 0), (w4_pass, 1), (dw_pass, 1))

        def gate(n, result, store_pieces=False):
            for lo, hi in ranges(GATE_PIECES[n]):
                nc.vector.tensor_tensor(result[:, lo:hi], gate_window[n][:].indirect(picks(lo, hi)), ys[n][:, lo:hi], MULT)
                if store_pieces:
                    nc.sync.dma_start(out[n * P : (n + 1) * P, lo:hi], result[:, lo:hi])

        first_two = tile([P, 2, S], F32, "result0")
        for one_pass, a in ((w4_pass, 0), (w4_pass, 1), (dw_pass, 0), (dw_pass, 1)):
            passes(one_pass, a, 0)
        copy_sums(0)
        gate(0, first_two[:, 0, :])
        late_sums(1, dw_first, (0,))
        late_sums(1, dw_first, (1,))
        for n in range(EARLY_DW, ROW_TILES):
            round_dw(0, n, nc.scalar.copy)
            quantize_dw(0, n)
        copy_sums(1)
        gate(1, first_two[:, 1, :])
        round_dw(1, 3, nc.scalar.copy)
        quantize_dw(1, 3)
        nc.sync.dma_start(out[: 2 * P, :].rearrange("(n p) j -> p n j", p=P), first_two[:])
        third = tile([P, S], F32, "result2")
        for n, order in ((2, pass_0_last), (3, pass_1_last)):
            for piece in range(len(SUM_PIECES[n])):
                late_sums(n, order, (piece,))
            copy_sums(n)
        gate(2, third[:])
        nc.sync.dma_start(out[2 * P : 3 * P, :], third[:])
        fourth = tile([P, S], F32, "result3")
        gate(3, fourth[:], True)
